import numpy as np
import ml_dtypes


def mxq(x, axis, fmt="e4m3"):
    dtype, down = {"e4m3": (ml_dtypes.float8_e4m3fn, 7), "e5m2": (ml_dtypes.float8_e5m2, 14)}[fmt]
    v = np.moveaxis(np.asarray(x, np.float32).astype(ml_dtypes.bfloat16).astype(np.float64), axis, -1)
    blocks = v.reshape(v.shape[:-1] + (-1, 32))
    amax = np.abs(blocks).max(-1, keepdims=True)
    byte = np.maximum(np.where(amax > 0, np.frexp(amax)[1] - 1 + 127, 0) - down, 1)
    scale = np.exp2(byte - 127.0)
    codes = (blocks / scale).astype(np.float32).astype(dtype).astype(np.float64)
    return np.moveaxis((codes * scale).reshape(v.shape), -1, axis)


WIDE = False


def mx_kscale(k):
    if not WIDE:
        return np.ones(k)
    levels = np.array([10, -10, 5, -5, 0])
    if k % 512:
        return np.exp2(np.random.permutation(np.resize(levels, k // 32))).repeat(32)
    a = np.empty((k // 512, 16))
    for p in range(k // 512):
        a[p, :8] = np.random.permutation(np.resize(levels, 8))
        for g in range(8):
            far = levels[np.abs(levels - a[p, g]) >= 10]
            a[p, g + 8] = far[np.random.randint(len(far))]
    return np.exp2(a.ravel()).repeat(32)


def f64(x):
    return np.asarray(x).astype(np.float64)


def striped(idx):
    return np.tile(idx.reshape(-1, 16).T, (8, 1)).astype(np.uint16)


def unstriped(offs):
    return offs[:16].T.reshape(-1).astype(np.int64)


E2M1 = np.array([0.0, 0.5, 1.0, 1.5, 2.0, 3.0, 4.0, 6.0, -0.0, -0.5, -1.0, -1.5, -2.0, -3.0, -4.0, -6.0])


def pack_weight(w, fmt):
    k, n = w.shape
    w = f64(np.asarray(w, np.float32).astype(ml_dtypes.bfloat16)).reshape(k // 32, 32, n)
    amax = np.abs(w).max(1)
    if fmt == "e4m3":
        byte = np.frexp(amax)[1] - 1 + 127 - 7
    else:
        mant, ex = np.frexp(amax / 6.0)
        byte = np.where(mant > 0.5, ex, ex - 1) + 127
    byte = np.clip(np.where(amax > 0, byte, 1), 1, 254)
    scaled = (w * np.exp2(127.0 - byte)[:, None, :]).reshape(k, n).astype(np.float32)
    by_word = np.ascontiguousarray(scaled.reshape(k // 512, 128, 4, n).transpose(0, 1, 3, 2))
    if fmt == "e4m3":
        words = by_word.astype(ml_dtypes.float8_e4m3fn).view(np.uint8)
    else:
        c = by_word.astype(ml_dtypes.float4_e2m1fn).view(np.uint8) & 0xF
        words = (c[..., 0::2] | (c[..., 1::2] << 4)).reshape(k // 512, 128, 2 * n)
    return np.ascontiguousarray(words), np.ascontiguousarray(byte.astype(np.uint8).reshape(k // 512, 16, n))


def unpack_weight(words, scales, fmt):
    g, _, n = scales.shape
    words = np.ascontiguousarray(words).reshape(g, 128, n, -1)
    if fmt == "e4m3":
        vals = words.view(ml_dtypes.float8_e4m3fn).astype(np.float64)
    else:
        nib = np.empty((g, 128, n, 4), np.uint8)
        nib[..., 0::2] = words & 0xF
        nib[..., 1::2] = words >> 4
        vals = E2M1[nib]
    vals = vals * np.repeat(np.exp2(scales.astype(np.float64) - 127.0), 8, axis=1)[..., None]
    return vals.transpose(0, 1, 3, 2).reshape(g * 512, n)


def relu2(v):
    return np.maximum(v, 0.0) ** 2


K, T, E, C, H, N = 1536, 2048, 4, 256, 512, 128


def by_expert(wq, xq):
    return np.concatenate([wq[e].T @ xq[:, e * C:(e + 1) * C] for e in range(E)], axis=1)


def setup_inputs():
    n = np.random.standard_normal
    s = mx_kscale(K)[:, None]
    u = mx_kscale(H)
    w1 = [pack_weight(m, "e2m1") for m in n((E, K, H)) / np.sqrt(K) / s[None] * u[None, None, :]]
    w2 = [pack_weight(m, "e2m1") for m in n((E, H, N)) / np.sqrt(H) / u[None, :, None] ** 2]
    x = pack_weight(n((K, T)) * s, "e4m3")
    return {
        "x_words": x[0],
        "x_scales": x[1],
        "w1_words": np.stack([m[0] for m in w1]),
        "w1_scales": np.stack([m[1] for m in w1]),
        "w2_words": np.stack([m[0] for m in w2]),
        "w2_scales": np.stack([m[1] for m in w2]),
        "gate": np.tile(np.random.uniform(0.2, 1.0, E * C), (N, 1)).astype(np.float32),
        "offs": striped(np.random.permutation(T)[:E * C]),
        "dst": striped(np.random.permutation(T)[:E * C]),
    }


def reference(x_words, x_scales, w1_words, w1_scales, w2_words, w2_scales, gate, offs, dst):
    idx = unstriped(offs)
    w1 = np.stack([unpack_weight(w1_words[e], w1_scales[e], "e2m1") for e in range(E)])
    w2 = np.stack([unpack_weight(w2_words[e], w2_scales[e], "e2m1") for e in range(E)])
    xq = unpack_weight(x_words, x_scales, "e4m3")[:, idx]
    h = relu2(by_expert(w1, xq))
    y = by_expert(w2, mxq(h, 0, "e4m3"))
    out = np.zeros((N, T))
    out[:, unstriped(dst)] = f64(gate) * y
    return out

@@ -1,0 +1,183 @@
+from contextlib import ExitStack
+
+import concourse.mybir as mybir
+from concourse.masks import make_identity
+
+K, T, E, C, H, N = 1536, 2048, 4, 256, 512, 128
+FLOPS = 2 * E * C * (K * H + H * N)
+
+F32 = mybir.dt.float32
+BF16 = mybir.dt.bfloat16
+I32 = mybir.dt.int32
+U32 = mybir.dt.uint32
+U16 = mybir.dt.uint16
+U8 = mybir.dt.uint8
+FP8X4 = mybir.dt.float8_e4m3fn_x4
+FP4X4 = mybir.dt.float4_e2m1fn_x4
+ACT = mybir.ActivationFunctionType
+MULT = mybir.AluOpType.mult
+
+P = 128
+PASSES = K // 512
+SLOTS = E * C
+TILES = SLOTS // P
+RELU_ON_VECTOR = (2, 3)
+
+
+def tile_moe_two_mlp_relu2_kernel(
+    tc, x_words, x_scales, w1_words, w1_scales, w2_words, w2_scales, gate, offs, dst, out
+):
+    nc = tc.nc
+    with ExitStack() as ctx:
+        keep = ctx.enter_context(tc.tile_pool(name="keep", bufs=1))
+        work = ctx.enter_context(tc.tile_pool(name="work", bufs=4))
+        psum_a = ctx.enter_context(tc.psum_pool(name="psum_a", bufs=4))
+        psum_t = ctx.enter_context(tc.psum_pool(name="psum_t", bufs=3))
+        psum_y = ctx.enter_context(tc.psum_pool(name="psum_y", bufs=1))
+
+        offs_t = keep.tile([P, SLOTS // 16], U16, name="offs_t")
+        dst_t = keep.tile([P, SLOTS // 16], U16, name="dst_t")
+        xs = keep.tile([P, T], U8, name="xs", align_bytes=64)
+        xw = [keep.tile([P, T], I32, name="xw%d" % o, align_bytes=64) for o in range(PASSES)]
+        gs = keep.tile([P, SLOTS], U8, name="gs", align_bytes=64)
+        planes = keep.tile([P, 4, SLOTS], U8, name="planes", align_bytes=64)
+        gw = [keep.tile([P, SLOTS], U32, name="gw%d" % o, align_bytes=64) for o in range(PASSES)]
+        w1w = keep.tile([P, E, PASSES, 2 * H], U8, name="w1w", align_bytes=64)
+        w1s = keep.tile([P, E * PASSES, H], U8, name="w1s", align_bytes=64)
+        w2w = keep.tile([P, E, 2 * N], U8, name="w2w", align_bytes=64)
+        w2s = keep.tile([P, E, N], U8, name="w2s", align_bytes=64)
+        gate_t = keep.tile([P, SLOTS], F32, name="gate_t")
+        placed = keep.tile([P, T], F32, name="placed")
+        zero = keep.tile([P, 8], F32, name="zero")
+        ident = keep.tile([P, P], F32, name="ident")
+        h_words = keep.tile([P, SLOTS], U32, name="h_words", align_bytes=64)
+        h_scales = keep.tile([P, SLOTS], U8, name="h_scales", align_bytes=64)
+
+        w1w_hbm = w1_words.rearrange("e s p b -> p e s b").bitcast(I32)
+        w1s_hbm = w1_scales.rearrange("e s q i -> q (e s) i").bitcast(I32)
+        w2w_hbm = w2_words.rearrange("e s p b -> p (e s) b").bitcast(I32)
+        w2s_hbm = w2_scales.rearrange("e s q n -> q (e s) n").bitcast(I32)
+
+        def load_x(o):
+            nc.sync.dma_start(xw[o][:], x_words[o].rearrange("p t r -> p (t r)").bitcast(I32))
+
+        def load_rows(plane, rows):
+            for q in range(4):
+                nc.gpsimd.dma_start(plane[32 * q : 32 * q + 4].bitcast(I32), rows[4 * q : 4 * q + 4])
+
+        nc.vector.memset(xs[:].bitcast(I32), 0)
+        nc.vector.memset(w1s[:].bitcast(I32), 0)
+        nc.vector.memset(zero[:], 0.0)
+        nc.vector.memset(w2s[:].bitcast(I32), 0)
+        nc.vector.memset(planes[:].bitcast(I32), 0)
+        make_identity(nc, ident[:])
+
+        nc.sync.dma_start(offs_t[:], offs)
+        for o in range(PASSES):
+            nc.scalar.dma_start(xs[o:64:4, :].bitcast(I32), x_scales[o].bitcast(I32))
+        load_x(0)
+        nc.sync.dma_start(dst_t[:], dst)
+        nc.sync.dma_start(w1w[:, 0:2, 0, :].bitcast(I32), w1w_hbm[:, 0:2, 0, :])
+        load_x(1)
+        nc.sync.dma_start(w1w[:, 0:2, 1, :].bitcast(I32), w1w_hbm[:, 0:2, 1, :])
+        load_x(2)
+        nc.sync.dma_start(w1w[:, 0:2, 2, :].bitcast(I32), w1w_hbm[:, 0:2, 2, :])
+        nc.sync.dma_start(w1w[:, 2, :, :].bitcast(I32), w1w_hbm[:, 2, :, :])
+        nc.sync.dma_start(w2w[:].bitcast(I32), w2w_hbm)
+        nc.sync.dma_start(gate_t[:], gate)
+        nc.sync.dma_start(w1w[:, 3, :, :].bitcast(I32), w1w_hbm[:, 3, :, :])
+        load_rows(w1s, w1s_hbm)
+        load_rows(w2s, w2s_hbm)
+
+        nc.scalar.activation(placed[:], zero[:, 0:1].to_broadcast([P, T]), ACT.Square)
+
+        def gather_words(o, lo, hi):
+            nc.vector.tensor_copy(
+                gw[o][:, lo:hi], xw[o][:].bitcast(U32).indirect(offs_t[:, lo // 16 : hi // 16])
+            )
+
+        nc.vector.tensor_copy(gs[:], xs[:].indirect(offs_t[:]))
+        for q in range(4):
+            nc.scalar.dma_start(
+                planes[32 * q : 32 * q + 4].bitcast(I32),
+                gs[16 * q : 16 * q + 16, :].bitcast(I32),
+            )
+        gather_words(0, 0, SLOTS)
+        gather_words(1, 0, SLOTS)
+        for e in range(E):
+            gather_words(2, e * C, (e + 1) * C)
+
+        sums = {}
+        relus = {}
+
+        def first_layer(j, o):
+            if o == 0:
+                sums[j] = psum_a.tile([P, H], F32, name="a")
+            e = j * P // C
+            cols = slice(j * P, (j + 1) * P)
+            nc.tensor.matmul_mx(
+                out=sums[j][:],
+                lhsT=gw[o][:, cols].bitcast(FP8X4),
+                lhsT_scale=planes[:, o, cols],
+                rhs=w1w[:, e, o, :].bitcast(FP4X4),
+                rhs_scale=w1s[:, e * PASSES + o, :],
+                start=(o == 0),
+                stop=(o == PASSES - 1),
+            )
+
+        def rectify(j):
+            relus[j] = work.tile([P, 4, P], F32, name="relu")
+            by_plane = sums[j][:].rearrange("s (p t) -> s t p", t=4)
+            if j in RELU_ON_VECTOR:
+                nc.vector.tensor_scalar_max(relus[j][:], by_plane, 0.0)
+            else:
+                nc.scalar.activation(relus[j][:], by_plane, ACT.Relu)
+
+        def turn_and_quantise(j):
+            cols = slice(j * P, (j + 1) * P)
+            turned = psum_t.tile([P, 4, P], F32, name="turned")
+            for t in range(4):
+                nc.tensor.transpose(turned[:, t, :], relus[j][:, t, :], ident[:])
+            h = work.tile([P, P, 4], BF16, name="h", align_bytes=64)
+            nc.scalar.activation(h[:], turned[:].rearrange("p t s -> p s t"), ACT.Square)
+            nc.vector.quantize_mx(
+                out=h_words[:, cols].bitcast(FP8X4),
+                scales=h_scales[:, cols],
+                in_=h[:].rearrange("p s t -> p (s t)"),
+            )
+
+        def second_layer(e):
+            cols = slice(e * C, (e + 1) * C)
+            y = psum_y.tile([P, C], F32, name="y")
+            nc.tensor.matmul_mx(
+                out=y[:],
+                lhsT=w2w[:, e, :].bitcast(FP4X4),
+                lhsT_scale=w2s[:, e, :],
+                rhs=h_words[:, cols].bitcast(FP8X4),
+                rhs_scale=h_scales[:, cols],
+                start=True,
+                stop=True,
+            )
+            y_sb = work.tile([P, C], F32, name="y_sb")
+            window = placed[:].indirect(dst_t[:, e * C // 16 : (e + 1) * C // 16])
+            nc.vector.tensor_tensor(y_sb[:], y[:], gate_t[:, cols], MULT)
+            nc.vector.tensor_copy(window, y_sb[:])
+
+        for o in range(PASSES - 1):
+            for j in range(4):
+                first_layer(j, o)
+        for j in range(4):
+            first_layer(j, PASSES - 1)
+            rectify(j)
+        for e in range(E):
+            turn_and_quantise(2 * e)
+            turn_and_quantise(2 * e + 1)
+            if e >= 1:
+                second_layer(e - 1)
+            for j in range(2 * e + 4, min(2 * e + 6, TILES)):
+                for o in range(PASSES):
+                    first_layer(j, o)
+                rectify(j)
+        second_layer(E - 1)
+
+        nc.sync.dma_start(out, placed[:])

@@ -37,17 +37,16 @@ def tile_moe_two_mlp_relu2_kernel(
 
         offs_t = keep.tile([P, SLOTS // 16], U16, name="offs_t")
         dst_t = keep.tile([P, SLOTS // 16], U16, name="dst_t")
-        xs = keep.tile([P, T], U8, name="xs", align_bytes=64)
+        xs = keep.tile([P, T], U8, name="xs", tag="window", align_bytes=64)
         xw = [keep.tile([P, T], I32, name="xw%d" % o, align_bytes=64) for o in range(PASSES)]
         gs = keep.tile([P, SLOTS], U8, name="gs", align_bytes=64)
         planes = keep.tile([P, 4, SLOTS], U8, name="planes", align_bytes=64)
         gw = [keep.tile([P, SLOTS], U32, name="gw%d" % o, align_bytes=64) for o in range(PASSES)]
         w1w = keep.tile([P, E, PASSES, 2 * H], U8, name="w1w", align_bytes=64)
-        w1s = keep.tile([P, E * PASSES, H], U8, name="w1s", align_bytes=64)
+        w1s = [keep.tile([P, 2 * PASSES, H], U8, name="w1s%d" % g, align_bytes=64) for g in range(2)]
         w2w = keep.tile([P, E, 2 * N], U8, name="w2w", align_bytes=64)
         w2s = keep.tile([P, E, N], U8, name="w2s", align_bytes=64)
         gate_t = keep.tile([P, SLOTS], F32, name="gate_t")
-        placed = keep.tile([P, T], F32, name="placed")
         zero = keep.tile([P, 8], F32, name="zero")
         ident = keep.tile([P, P], F32, name="ident")
         h_words = keep.tile([P, SLOTS], U32, name="h_words", align_bytes=64)
@@ -61,35 +60,38 @@ def tile_moe_two_mlp_relu2_kernel(
         def load_x(o):
             nc.sync.dma_start(xw[o][:], x_words[o].rearrange("p t r -> p (t r)").bitcast(I32))
 
-        def load_rows(plane, rows):
+        def load_rows(queue, plane, rows):
             for q in range(4):
-                nc.gpsimd.dma_start(plane[32 * q : 32 * q + 4].bitcast(I32), rows[4 * q : 4 * q + 4])
+                queue.dma_start(plane[32 * q : 32 * q + 4].bitcast(I32), rows[4 * q : 4 * q + 4])
 
         nc.vector.memset(xs[:].bitcast(I32), 0)
-        nc.vector.memset(w1s[:].bitcast(I32), 0)
-        nc.vector.memset(zero[:], 0.0)
-        nc.vector.memset(w2s[:].bitcast(I32), 0)
+        nc.vector.memset(w1s[0][:].bitcast(I32), 0)
         nc.vector.memset(planes[:].bitcast(I32), 0)
+        nc.vector.memset(w1s[1][:].bitcast(I32), 0)
+        nc.vector.memset(w2s[:].bitcast(I32), 0)
+        nc.vector.memset(zero[:], 0.0)
         make_identity(nc, ident[:])
+
+        def load_w1(experts, passes):
+            nc.sync.dma_start(w1w[:, experts, passes, :].bitcast(I32), w1w_hbm[:, experts, passes, :])
 
         nc.sync.dma_start(offs_t[:], offs)
         for o in range(PASSES):
             nc.scalar.dma_start(xs[o:64:4, :].bitcast(I32), x_scales[o].bitcast(I32))
+        load_rows(nc.scalar, w1s[0], w1s_hbm[:, 0 : 2 * PASSES, :])
         load_x(0)
-        nc.sync.dma_start(dst_t[:], dst)
-        nc.sync.dma_start(w1w[:, 0:2, 0, :].bitcast(I32), w1w_hbm[:, 0:2, 0, :])
+        load_w1(slice(0, 2), 0)
         load_x(1)
-        nc.sync.dma_start(w1w[:, 0:2, 1, :].bitcast(I32), w1w_hbm[:, 0:2, 1, :])
+        load_w1(slice(0, 2), 1)
         load_x(2)
-        nc.sync.dma_start(w1w[:, 0:2, 2, :].bitcast(I32), w1w_hbm[:, 0:2, 2, :])
-        nc.sync.dma_start(w1w[:, 2, :, :].bitcast(I32), w1w_hbm[:, 2, :, :])
+        load_w1(slice(0, 2), 2)
+        nc.sync.dma_start(dst_t[:], dst)
+        load_rows(nc.sync, w1s[1], w1s_hbm[:, 2 * PASSES : 4 * PASSES, :])
+        load_w1(2, slice(0, PASSES))
         nc.sync.dma_start(w2w[:].bitcast(I32), w2w_hbm)
+        load_w1(3, slice(0, PASSES))
+        load_rows(nc.sync, w2s, w2s_hbm)
         nc.sync.dma_start(gate_t[:], gate)
-        nc.sync.dma_start(w1w[:, 3, :, :].bitcast(I32), w1w_hbm[:, 3, :, :])
-        load_rows(w1s, w1s_hbm)
-        load_rows(w2s, w2s_hbm)
-
-        nc.scalar.activation(placed[:], zero[:, 0:1].to_broadcast([P, T]), ACT.Square)
 
         def gather_words(o, lo, hi):
             nc.vector.tensor_copy(
@@ -102,6 +104,8 @@ def tile_moe_two_mlp_relu2_kernel(
                 planes[32 * q : 32 * q + 4].bitcast(I32),
                 gs[16 * q : 16 * q + 16, :].bitcast(I32),
             )
+        placed = keep.tile([P, T], F32, name="placed", tag="window", align_bytes=64)
+        nc.scalar.activation(placed[:], zero[:, 0:1].to_broadcast([P, T]), ACT.Square)
         gather_words(0, 0, SLOTS)
         gather_words(1, 0, SLOTS)
         for e in range(E):
@@ -120,7 +124,7 @@ def tile_moe_two_mlp_relu2_kernel(
                 lhsT=gw[o][:, cols].bitcast(FP8X4),
                 lhsT_scale=planes[:, o, cols],
                 rhs=w1w[:, e, o, :].bitcast(FP4X4),
-                rhs_scale=w1s[:, e * PASSES + o, :],
+                rhs_scale=w1s[e // 2][:, (e % 2) * PASSES + o, :],
                 start=(o == 0),
                 stop=(o == PASSES - 1),
             )
@@ -160,8 +164,8 @@ def tile_moe_two_mlp_relu2_kernel(
             )
             y_sb = work.tile([P, C], F32, name="y_sb")
             window = placed[:].indirect(dst_t[:, e * C // 16 : (e + 1) * C // 16])
-            nc.vector.tensor_tensor(y_sb[:], y[:], gate_t[:, cols], MULT)
-            nc.vector.tensor_copy(window, y_sb[:])
+            nc.scalar.copy(y_sb[:], y[:])
+            nc.vector.tensor_tensor(window, y_sb[:], gate_t[:, cols], MULT)
 
         for o in range(PASSES - 1):
             for j in range(4):
@@ -172,12 +176,10 @@ def tile_moe_two_mlp_relu2_kernel(
         for e in range(E):
             turn_and_quantise(2 * e)
             turn_and_quantise(2 * e + 1)
-            if e >= 1:
-                second_layer(e - 1)
+            second_layer(e)
             for j in range(2 * e + 4, min(2 * e + 6, TILES)):
                 for o in range(PASSES):
                     first_layer(j, o)
                 rectify(j)
-        second_layer(E - 1)
 
         nc.sync.dma_start(out, placed[:])

@@ -21,7 +21,9 @@ P = 128
 PASSES = K // 512
 SLOTS = E * C
 TILES = SLOTS // P
-RELU_ON_VECTOR = (2, 3)
+ON_VECTOR = ["R1","R3","R4"]
+BANK = {"a0":0,"a1":1,"a2":2,"a3":3,"t0":4,"t1":5,"t2":6,"t3":7,"a4":0,"a5":1,"y0":2,"a6":3,"y1":4,"a7":5,"t4":6,"t5":7,"t6":0,"t7":1,"y2":0,"y3":2}
+ORDER = "G0 G1 G2 M0 R0 M1 R1 M2 R2 M3 R3 G3 T0 S0 Q0 T1 S1 Q1 T2 S2 Q2 T3 S3 Q3 L4 M4 L5 Y0 C0 R4 M5 R5 X0 L6 M6 R6 Y1 C1 X1 L7 M7 R7 T4 S4 Q4 T5 S5 Q5 T6 S6 Q6 T7 S7 Q7 Y2 C2 X2 Y3 C3 X3".split()
 
 
 def tile_moe_two_mlp_relu2_kernel(
@@ -30,20 +32,17 @@ def tile_moe_two_mlp_relu2_kernel(
     nc = tc.nc
     with ExitStack() as ctx:
         keep = ctx.enter_context(tc.tile_pool(name="keep", bufs=1))
-        work = ctx.enter_context(tc.tile_pool(name="work", bufs=4))
-        psum_a = ctx.enter_context(tc.psum_pool(name="psum_a", bufs=4))
-        psum_t = ctx.enter_context(tc.psum_pool(name="psum_t", bufs=3))
-        psum_y = ctx.enter_context(tc.psum_pool(name="psum_y", bufs=1))
+        psum = ctx.enter_context(tc.psum_pool(name="psum", bufs=1))
 
         offs_t = keep.tile([P, SLOTS // 16], U16, name="offs_t")
         dst_t = keep.tile([P, SLOTS // 16], U16, name="dst_t")
         xs = keep.tile([P, T], U8, name="xs", tag="window", align_bytes=64)
         xw = [keep.tile([P, T], I32, name="xw%d" % o, align_bytes=64) for o in range(PASSES)]
-        gs = keep.tile([P, SLOTS], U8, name="gs", align_bytes=64)
+        gs = keep.tile([P, SLOTS], U8, name="gs", tag="scales", align_bytes=64)
         planes = keep.tile([P, 4, SLOTS], U8, name="planes", align_bytes=64)
         gw = [keep.tile([P, SLOTS], U32, name="gw%d" % o, align_bytes=64) for o in range(PASSES)]
         w1w = keep.tile([P, E, PASSES, 2 * H], U8, name="w1w", align_bytes=64)
-        w1s = [keep.tile([P, 2 * PASSES, H], U8, name="w1s%d" % g, align_bytes=64) for g in range(2)]
+        w1s = [keep.tile([P, 2 * PASSES, H], U8, name="w1s_first", align_bytes=64)]
         w2w = keep.tile([P, E, 2 * N], U8, name="w2w", align_bytes=64)
         w2s = keep.tile([P, E, N], U8, name="w2s", align_bytes=64)
         gate_t = keep.tile([P, SLOTS], F32, name="gate_t")
@@ -60,14 +59,13 @@ def tile_moe_two_mlp_relu2_kernel(
         def load_x(o):
             nc.sync.dma_start(xw[o][:], x_words[o].rearrange("p t r -> p (t r)").bitcast(I32))
 
-        def load_rows(queue, plane, rows):
-            for q in range(4):
-                queue.dma_start(plane[32 * q : 32 * q + 4].bitcast(I32), rows[4 * q : 4 * q + 4])
+        def load_rows(plane, rows, queue=nc.sync):
+            for r in range(4):
+                queue.dma_start(plane[r:P:32].bitcast(I32), rows[r:16:4])
 
         nc.vector.memset(xs[:].bitcast(I32), 0)
         nc.vector.memset(w1s[0][:].bitcast(I32), 0)
         nc.vector.memset(planes[:].bitcast(I32), 0)
-        nc.vector.memset(w1s[1][:].bitcast(I32), 0)
         nc.vector.memset(w2s[:].bitcast(I32), 0)
         nc.vector.memset(zero[:], 0.0)
         make_identity(nc, ident[:])
@@ -76,47 +74,47 @@ def tile_moe_two_mlp_relu2_kernel(
             nc.sync.dma_start(w1w[:, experts, passes, :].bitcast(I32), w1w_hbm[:, experts, passes, :])
 
         nc.sync.dma_start(offs_t[:], offs)
+        nc.sync.dma_start(dst_t[:], dst)
         for o in range(PASSES):
-            nc.scalar.dma_start(xs[o:64:4, :].bitcast(I32), x_scales[o].bitcast(I32))
-        load_rows(nc.scalar, w1s[0], w1s_hbm[:, 0 : 2 * PASSES, :])
+            nc.scalar.dma_start(
+                xs[o:64:4, :].bitcast(I32),
+                x_scales[o].rearrange("(q r) t -> r q t", r=4).bitcast(I32),
+            )
         load_x(0)
-        load_w1(slice(0, 2), 0)
+        load_rows(w1s[0], w1s_hbm[:, 0 : 2 * PASSES, :])
         load_x(1)
+        load_w1(slice(0, 2), 0)
+        nc.vector.tensor_copy(gs[:], xs[:].indirect(offs_t[:]))
+        for r in range(4):
+            nc.sync.dma_start(planes[r:P:32].bitcast(I32), gs[16 * r : 16 * r + 16, :].bitcast(I32))
         load_w1(slice(0, 2), 1)
         load_x(2)
         load_w1(slice(0, 2), 2)
-        nc.sync.dma_start(dst_t[:], dst)
-        load_rows(nc.sync, w1s[1], w1s_hbm[:, 2 * PASSES : 4 * PASSES, :])
         load_w1(2, slice(0, PASSES))
         nc.sync.dma_start(w2w[:].bitcast(I32), w2w_hbm)
+        load_rows(w2s, w2s_hbm)
         load_w1(3, slice(0, PASSES))
-        load_rows(nc.sync, w2s, w2s_hbm)
         nc.sync.dma_start(gate_t[:], gate)
+
+        placed = keep.tile([P, T], F32, name="placed", tag="window", align_bytes=64)
+        nc.scalar.activation(placed[:], zero[:, 0:1].to_broadcast([P, T]), ACT.Square)
 
         def gather_words(o, lo, hi):
             nc.vector.tensor_copy(
                 gw[o][:, lo:hi], xw[o][:].bitcast(U32).indirect(offs_t[:, lo // 16 : hi // 16])
             )
 
-        nc.vector.tensor_copy(gs[:], xs[:].indirect(offs_t[:]))
-        for q in range(4):
-            nc.scalar.dma_start(
-                planes[32 * q : 32 * q + 4].bitcast(I32),
-                gs[16 * q : 16 * q + 16, :].bitcast(I32),
-            )
-        placed = keep.tile([P, T], F32, name="placed", tag="window", align_bytes=64)
-        nc.scalar.activation(placed[:], zero[:, 0:1].to_broadcast([P, T]), ACT.Square)
         gather_words(0, 0, SLOTS)
         gather_words(1, 0, SLOTS)
-        for e in range(E):
-            gather_words(2, e * C, (e + 1) * C)
+        w1s.append(keep.tile([P, 2 * PASSES, H], U8, name="w1s_second", tag="scales", align_bytes=64))
+        nc.vector.memset(w1s[1][:].bitcast(I32), 0)
+        load_rows(w1s[1], w1s_hbm[:, 2 * PASSES : 4 * PASSES, :], nc.scalar)
 
-        sums = {}
-        relus = {}
+        sums, relus, turned, h, y, y_sb = {}, {}, {}, {}, {}, {}
 
         def first_layer(j, o):
             if o == 0:
-                sums[j] = psum_a.tile([P, H], F32, name="a")
+                sums[j] = psum.tile([P, H], F32, name="sums", tag="bank%d" % BANK["a%d" % j])
             e = j * P // C
             cols = slice(j * P, (j + 1) * P)
             nc.tensor.matmul_mx(
@@ -129,57 +127,61 @@ def tile_moe_two_mlp_relu2_kernel(
                 stop=(o == PASSES - 1),
             )
 
-        def rectify(j):
-            relus[j] = work.tile([P, 4, P], F32, name="relu")
-            by_plane = sums[j][:].rearrange("s (p t) -> s t p", t=4)
-            if j in RELU_ON_VECTOR:
-                nc.vector.tensor_scalar_max(relus[j][:], by_plane, 0.0)
-            else:
-                nc.scalar.activation(relus[j][:], by_plane, ACT.Relu)
-
-        def turn_and_quantise(j):
+        def step(kind, j):
             cols = slice(j * P, (j + 1) * P)
-            turned = psum_t.tile([P, 4, P], F32, name="turned")
-            for t in range(4):
-                nc.tensor.transpose(turned[:, t, :], relus[j][:, t, :], ident[:])
-            h = work.tile([P, P, 4], BF16, name="h", align_bytes=64)
-            nc.scalar.activation(h[:], turned[:].rearrange("p t s -> p s t"), ACT.Square)
-            nc.vector.quantize_mx(
-                out=h_words[:, cols].bitcast(FP8X4),
-                scales=h_scales[:, cols],
-                in_=h[:].rearrange("p s t -> p (s t)"),
-            )
-
-        def second_layer(e):
-            cols = slice(e * C, (e + 1) * C)
-            y = psum_y.tile([P, C], F32, name="y")
-            nc.tensor.matmul_mx(
-                out=y[:],
-                lhsT=w2w[:, e, :].bitcast(FP4X4),
-                lhsT_scale=w2s[:, e, :],
-                rhs=h_words[:, cols].bitcast(FP8X4),
-                rhs_scale=h_scales[:, cols],
-                start=True,
-                stop=True,
-            )
-            y_sb = work.tile([P, C], F32, name="y_sb")
-            window = placed[:].indirect(dst_t[:, e * C // 16 : (e + 1) * C // 16])
-            nc.scalar.copy(y_sb[:], y[:])
-            nc.vector.tensor_tensor(window, y_sb[:], gate_t[:, cols], MULT)
+            slots = slice(j * C, (j + 1) * C)
+            if kind == "G":
+                gather_words(2, j * C, (j + 1) * C)
+            elif kind == "L":
+                first_layer(j, 0)
+                first_layer(j, 1)
+            elif kind == "M":
+                first_layer(j, 2)
+            elif kind == "R":
+                relus[j] = keep.tile([P, 4, P], F32, name="relu%d" % j)
+                by_plane = sums[j][:].rearrange("s (p t) -> s t p", t=4)
+                if "R%d" % j in ON_VECTOR:
+                    nc.vector.tensor_scalar_max(relus[j][:], by_plane, 0.0)
+                else:
+                    nc.scalar.activation(relus[j][:], by_plane, ACT.Relu)
+            elif kind == "T":
+                turned[j] = psum.tile([P, 4, P], F32, name="turned", tag="bank%d" % BANK["t%d" % j])
+                for t in range(4):
+                    nc.tensor.transpose(turned[j][:, t, :], relus[j][:, t, :], ident[:])
+            elif kind == "S":
+                h[j] = keep.tile([P, P, 4], BF16, name="h%d" % j, align_bytes=64)
+                nc.scalar.activation(h[j][:], turned[j][:].rearrange("p t s -> p s t"), ACT.Square)
+            elif kind == "Q":
+                nc.vector.quantize_mx(
+                    out=h_words[:, cols].bitcast(FP8X4),
+                    scales=h_scales[:, cols],
+                    in_=h[j][:].rearrange("p s t -> p (s t)"),
+                )
+            elif kind == "Y":
+                y[j] = psum.tile([P, C], F32, name="y", tag="bank%d" % BANK["y%d" % j])
+                nc.tensor.matmul_mx(
+                    out=y[j][:],
+                    lhsT=w2w[:, j, :].bitcast(FP4X4),
+                    lhsT_scale=w2s[:, j, :],
+                    rhs=h_words[:, slots].bitcast(FP8X4),
+                    rhs_scale=h_scales[:, slots],
+                    start=True,
+                    stop=True,
+                )
+            elif kind == "C":
+                y_sb[j] = keep.tile([P, C], F32, name="y_sb%d" % j)
+                if "C%d" % j in ON_VECTOR:
+                    nc.vector.tensor_copy(y_sb[j][:], y[j][:])
+                else:
+                    nc.scalar.copy(y_sb[j][:], y[j][:])
+            else:
+                window = placed[:].indirect(dst_t[:, j * C // 16 : (j + 1) * C // 16])
+                nc.vector.tensor_tensor(window, y_sb[j][:], gate_t[:, slots], MULT)
 
         for o in range(PASSES - 1):
             for j in range(4):
                 first_layer(j, o)
-        for j in range(4):
-            first_layer(j, PASSES - 1)
-            rectify(j)
-        for e in range(E):
-            turn_and_quantise(2 * e)
-            turn_and_quantise(2 * e + 1)
-            second_layer(e)
-            for j in range(2 * e + 4, min(2 * e + 6, TILES)):
-                for o in range(PASSES):
-                    first_layer(j, o)
-                rectify(j)
+        for name in ORDER:
+            step(name[0], int(name[1]))
 
         nc.sync.dma_start(out, placed[:])

@@ -21,9 +21,8 @@ P = 128
 PASSES = K // 512
 SLOTS = E * C
 TILES = SLOTS // P
-ON_VECTOR = ["R1","R3","R4"]
-BANK = {"a0":0,"a1":1,"a2":2,"a3":3,"t0":4,"t1":5,"t2":6,"t3":7,"a4":0,"a5":1,"y0":2,"a6":3,"y1":4,"a7":5,"t4":6,"t5":7,"t6":0,"t7":1,"y2":0,"y3":2}
-ORDER = "G0 G1 G2 M0 R0 M1 R1 M2 R2 M3 R3 G3 T0 S0 Q0 T1 S1 Q1 T2 S2 Q2 T3 S3 Q3 L4 M4 L5 Y0 C0 R4 M5 R5 X0 L6 M6 R6 Y1 C1 X1 L7 M7 R7 T4 S4 Q4 T5 S5 Q5 T6 S6 Q6 T7 S7 Q7 Y2 C2 X2 Y3 C3 X3".split()
+HALF = SLOTS // 2
+RELU_ON_VECTOR = (1, 3, 5)
 
 
 def tile_moe_two_mlp_relu2_kernel(
@@ -40,9 +39,9 @@ def tile_moe_two_mlp_relu2_kernel(
         xw = [keep.tile([P, T], I32, name="xw%d" % o, align_bytes=64) for o in range(PASSES)]
         gs = keep.tile([P, SLOTS], U8, name="gs", tag="scales", align_bytes=64)
         planes = keep.tile([P, 4, SLOTS], U8, name="planes", align_bytes=64)
-        gw = [keep.tile([P, SLOTS], U32, name="gw%d" % o, align_bytes=64) for o in range(PASSES)]
+        gw = {}
         w1w = keep.tile([P, E, PASSES, 2 * H], U8, name="w1w", align_bytes=64)
-        w1s = [keep.tile([P, 2 * PASSES, H], U8, name="w1s_first", align_bytes=64)]
+        w1s = [keep.tile([P, 2 * PASSES, H], U8, name="w1s%d" % g, align_bytes=64) for g in range(2)]
         w2w = keep.tile([P, E, 2 * N], U8, name="w2w", align_bytes=64)
         w2s = keep.tile([P, E, N], U8, name="w2s", align_bytes=64)
         gate_t = keep.tile([P, SLOTS], F32, name="gate_t")
@@ -59,129 +58,156 @@ def tile_moe_two_mlp_relu2_kernel(
         def load_x(o):
             nc.sync.dma_start(xw[o][:], x_words[o].rearrange("p t r -> p (t r)").bitcast(I32))
 
-        def load_rows(plane, rows, queue=nc.sync):
-            for r in range(4):
-                queue.dma_start(plane[r:P:32].bitcast(I32), rows[r:16:4])
-
-        nc.vector.memset(xs[:].bitcast(I32), 0)
-        nc.vector.memset(w1s[0][:].bitcast(I32), 0)
-        nc.vector.memset(planes[:].bitcast(I32), 0)
-        nc.vector.memset(w2s[:].bitcast(I32), 0)
-        nc.vector.memset(zero[:], 0.0)
-        make_identity(nc, ident[:])
-
         def load_w1(experts, passes):
             nc.sync.dma_start(w1w[:, experts, passes, :].bitcast(I32), w1w_hbm[:, experts, passes, :])
 
+        def load_rows(plane, rows, queue, which=range(4)):
+            for r in which:
+                queue.dma_start(plane[r:P:32].bitcast(I32), rows[r:16:4])
+
+        def entries(lo, hi):
+            return slice(lo // 16, hi // 16)
+
+        def gather_words(o, g, pieces, tag):
+            gw[o, g] = keep.tile([P, HALF], U32, name="gw", tag=tag, align_bytes=64)
+            width = HALF // pieces
+            for lo in range(0, HALF, width):
+                chosen = offs_t[:, entries(g * HALF + lo, g * HALF + lo + width)]
+                nc.vector.tensor_copy(gw[o, g][:, lo : lo + width], xw[o][:].bitcast(U32).indirect(chosen))
+
+        for plane in (xs, w1s[0], w2s, planes, w1s[1]):
+            nc.vector.memset(plane[:].bitcast(I32), 0)
+        nc.vector.memset(zero[:], 0.0)
+        make_identity(nc, ident[:])
+
         nc.sync.dma_start(offs_t[:], offs)
-        nc.sync.dma_start(dst_t[:], dst)
         for o in range(PASSES):
             nc.scalar.dma_start(
-                xs[o:64:4, :].bitcast(I32),
+                xs[2 * o : P : 8, :].bitcast(I32),
                 x_scales[o].rearrange("(q r) t -> r q t", r=4).bitcast(I32),
             )
         load_x(0)
-        load_rows(w1s[0], w1s_hbm[:, 0 : 2 * PASSES, :])
+        load_rows(w1s[0], w1s_hbm[:, 0 : 2 * PASSES, :], nc.sync, range(0, 2))
         load_x(1)
+        load_rows(w1s[0], w1s_hbm[:, 0 : 2 * PASSES, :], nc.sync, range(2, 4))
+        load_rows(w2s, w2s_hbm, nc.sync)
         load_w1(slice(0, 2), 0)
         nc.vector.tensor_copy(gs[:], xs[:].indirect(offs_t[:]))
         for r in range(4):
-            nc.sync.dma_start(planes[r:P:32].bitcast(I32), gs[16 * r : 16 * r + 16, :].bitcast(I32))
+            nc.sync.dma_start(planes[r:P:32].bitcast(I32), gs[32 * r : 32 * r + 32 : 2, :].bitcast(I32))
         load_w1(slice(0, 2), 1)
         load_x(2)
         load_w1(slice(0, 2), 2)
+        load_rows(w1s[1], w1s_hbm[:, 2 * PASSES : 4 * PASSES, :], nc.sync)
         load_w1(2, slice(0, PASSES))
-        nc.sync.dma_start(w2w[:].bitcast(I32), w2w_hbm)
-        load_rows(w2s, w2s_hbm)
         load_w1(3, slice(0, PASSES))
+        nc.sync.dma_start(w2w[:].bitcast(I32), w2w_hbm)
+        nc.sync.dma_start(dst_t[:], dst)
         nc.sync.dma_start(gate_t[:], gate)
 
         placed = keep.tile([P, T], F32, name="placed", tag="window", align_bytes=64)
         nc.scalar.activation(placed[:], zero[:, 0:1].to_broadcast([P, T]), ACT.Square)
 
-        def gather_words(o, lo, hi):
-            nc.vector.tensor_copy(
-                gw[o][:, lo:hi], xw[o][:].bitcast(U32).indirect(offs_t[:, lo // 16 : hi // 16])
-            )
-
-        gather_words(0, 0, SLOTS)
-        gather_words(1, 0, SLOTS)
-        w1s.append(keep.tile([P, 2 * PASSES, H], U8, name="w1s_second", tag="scales", align_bytes=64))
-        nc.vector.memset(w1s[1][:].bitcast(I32), 0)
-        load_rows(w1s[1], w1s_hbm[:, 2 * PASSES : 4 * PASSES, :], nc.scalar)
-
-        sums, relus, turned, h, y, y_sb = {}, {}, {}, {}, {}, {}
+        sums, relus, h, y_sb = {}, {}, {}, {}
 
         def first_layer(j, o):
             if o == 0:
-                sums[j] = psum.tile([P, H], F32, name="sums", tag="bank%d" % BANK["a%d" % j])
+                sums[j] = psum.tile([P, H], F32, name="sums", tag="bank%d" % j)
             e = j * P // C
-            cols = slice(j * P, (j + 1) * P)
             nc.tensor.matmul_mx(
                 out=sums[j][:],
-                lhsT=gw[o][:, cols].bitcast(FP8X4),
-                lhsT_scale=planes[:, o, cols],
+                lhsT=gw[o, j * P // HALF][:, j * P % HALF : j * P % HALF + P].bitcast(FP8X4),
+                lhsT_scale=planes[:, o, j * P : (j + 1) * P],
                 rhs=w1w[:, e, o, :].bitcast(FP4X4),
                 rhs_scale=w1s[e // 2][:, (e % 2) * PASSES + o, :],
                 start=(o == 0),
                 stop=(o == PASSES - 1),
             )
 
-        def step(kind, j):
-            cols = slice(j * P, (j + 1) * P)
-            slots = slice(j * C, (j + 1) * C)
-            if kind == "G":
-                gather_words(2, j * C, (j + 1) * C)
-            elif kind == "L":
-                first_layer(j, 0)
-                first_layer(j, 1)
-            elif kind == "M":
-                first_layer(j, 2)
-            elif kind == "R":
-                relus[j] = keep.tile([P, 4, P], F32, name="relu%d" % j)
-                by_plane = sums[j][:].rearrange("s (p t) -> s t p", t=4)
-                if "R%d" % j in ON_VECTOR:
-                    nc.vector.tensor_scalar_max(relus[j][:], by_plane, 0.0)
-                else:
-                    nc.scalar.activation(relus[j][:], by_plane, ACT.Relu)
-            elif kind == "T":
-                turned[j] = psum.tile([P, 4, P], F32, name="turned", tag="bank%d" % BANK["t%d" % j])
-                for t in range(4):
-                    nc.tensor.transpose(turned[j][:, t, :], relus[j][:, t, :], ident[:])
-            elif kind == "S":
-                h[j] = keep.tile([P, P, 4], BF16, name="h%d" % j, align_bytes=64)
-                nc.scalar.activation(h[j][:], turned[j][:].rearrange("p t s -> p s t"), ACT.Square)
-            elif kind == "Q":
-                nc.vector.quantize_mx(
-                    out=h_words[:, cols].bitcast(FP8X4),
-                    scales=h_scales[:, cols],
-                    in_=h[j][:].rearrange("p s t -> p (s t)"),
-                )
-            elif kind == "Y":
-                y[j] = psum.tile([P, C], F32, name="y", tag="bank%d" % BANK["y%d" % j])
-                nc.tensor.matmul_mx(
-                    out=y[j][:],
-                    lhsT=w2w[:, j, :].bitcast(FP4X4),
-                    lhsT_scale=w2s[:, j, :],
-                    rhs=h_words[:, slots].bitcast(FP8X4),
-                    rhs_scale=h_scales[:, slots],
-                    start=True,
-                    stop=True,
-                )
-            elif kind == "C":
-                y_sb[j] = keep.tile([P, C], F32, name="y_sb%d" % j)
-                if "C%d" % j in ON_VECTOR:
-                    nc.vector.tensor_copy(y_sb[j][:], y[j][:])
-                else:
-                    nc.scalar.copy(y_sb[j][:], y[j][:])
+        def relu(j):
+            relus[j] = keep.tile([P, 4, P], F32, name="relu", tag="relu%d" % j, align_bytes=64)
+            by_plane = sums[j][:].rearrange("s (p t) -> s t p", t=4)
+            if j in RELU_ON_VECTOR:
+                nc.vector.tensor_scalar_max(relus[j][:], by_plane, 0.0)
             else:
-                window = placed[:].indirect(dst_t[:, j * C // 16 : (j + 1) * C // 16])
-                nc.vector.tensor_tensor(window, y_sb[j][:], gate_t[:, slots], MULT)
+                nc.scalar.activation(relus[j][:], by_plane, ACT.Relu)
+
+        def turn_and_square(j):
+            e = j * P // C
+            if j % 2 == 0:
+                h[e] = keep.tile([P, C, 4], BF16, name="h%d" % e, align_bytes=64)
+            turned = psum.tile([P, 4, P], F32, name="turned", tag="bank%d" % j)
+            for t in range(4):
+                nc.tensor.transpose(turned[:, t, :], relus[j][:, t, :], ident[:])
+            nc.scalar.activation(
+                h[e][:, (j % 2) * P : (j % 2 + 1) * P, :], turned[:].rearrange("p t s -> p s t"), ACT.Square
+            )
+
+        def quantise(e):
+            slots = slice(e * C, (e + 1) * C)
+            nc.vector.quantize_mx(
+                out=h_words[:, slots].bitcast(FP8X4),
+                scales=h_scales[:, slots],
+                in_=h[e][:].rearrange("p s t -> p (s t)"),
+            )
+
+        def second_layer(e):
+            slots = slice(e * C, (e + 1) * C)
+            y = psum.tile([P, C], F32, name="y", tag="bank%d" % (2 * e))
+            nc.tensor.matmul_mx(
+                out=y[:],
+                lhsT=w2w[:, e, :].bitcast(FP4X4),
+                lhsT_scale=w2s[:, e, :],
+                rhs=h_words[:, slots].bitcast(FP8X4),
+                rhs_scale=h_scales[:, slots],
+                start=True,
+                stop=True,
+            )
+            y_sb[e] = keep.tile([P, C], F32, name="y_sb", tag="relu%d" % ((2 * e + 3) % TILES), align_bytes=64)
+            nc.scalar.copy(y_sb[e][:], y[:])
+
+        def scatter(e):
+            window = placed[:].indirect(dst_t[:, entries(e * C, (e + 1) * C)])
+            nc.vector.tensor_tensor(window, y_sb[e][:], gate_t[:, e * C : (e + 1) * C], MULT)
 
         for o in range(PASSES - 1):
-            for j in range(4):
+            for g in range(2):
+                gather_words(o, g, 1, "gw%d%d" % (o, g))
+            for j in range(TILES // 2):
                 first_layer(j, o)
-        for name in ORDER:
-            step(name[0], int(name[1]))
+
+        def finish_sums(j):
+            for o in range(PASSES - 1 if j < TILES // 2 else 0, PASSES):
+                first_layer(j, o)
+            relu(j)
+
+        def hidden(e):
+            turn_and_square(2 * e + 1)
+            quantise(e)
+
+        def results(e):
+            second_layer(e)
+            scatter(e)
+
+        gather_words(PASSES - 1, 0, 2, "gw20")
+        for j in range(TILES // 2):
+            finish_sums(j)
+        turn_and_square(0)
+        gather_words(PASSES - 1, 1, 2, "relu0")
+        hidden(0)
+        turn_and_square(2)
+        hidden(1)
+        finish_sums(4)
+        finish_sums(5)
+        results(0)
+        finish_sums(6)
+        turn_and_square(4)
+        hidden(2)
+        results(1)
+        finish_sums(7)
+        turn_and_square(6)
+        hidden(3)
+        results(2)
+        results(3)
 
         nc.sync.dma_start(out, placed[:])

@@ -37,8 +37,8 @@ def tile_moe_two_mlp_relu2_kernel(
         dst_t = keep.tile([P, SLOTS // 16], U16, name="dst_t")
         xs = keep.tile([P, T], U8, name="xs", tag="window", align_bytes=64)
         xw = [keep.tile([P, T], I32, name="xw%d" % o, align_bytes=64) for o in range(PASSES)]
-        gs = keep.tile([P, SLOTS], U8, name="gs", tag="scales", align_bytes=64)
-        planes = keep.tile([P, 4, SLOTS], U8, name="planes", align_bytes=64)
+        gs = [keep.tile([P, HALF], U8, name="gs%d" % g, align_bytes=64) for g in range(2)]
+        planes = [keep.tile([P, 4, HALF], U8, name="planes%d" % g, align_bytes=64) for g in range(2)]
         gw = {}
         w1w = keep.tile([P, E, PASSES, 2 * H], U8, name="w1w", align_bytes=64)
         w1s = [keep.tile([P, 2 * PASSES, H], U8, name="w1s%d" % g, align_bytes=64) for g in range(2)]
@@ -61,9 +61,13 @@ def tile_moe_two_mlp_relu2_kernel(
         def load_w1(experts, passes):
             nc.sync.dma_start(w1w[:, experts, passes, :].bitcast(I32), w1w_hbm[:, experts, passes, :])
 
-        def load_rows(plane, rows, queue, which=range(4)):
-            for r in which:
+        def load_rows(plane, rows, queue):
+            for r in range(4):
                 queue.dma_start(plane[r:P:32].bitcast(I32), rows[r:16:4])
+
+        def move_planes(g):
+            for r in range(4):
+                nc.sync.dma_start(planes[g][r:P:32].bitcast(I32), gs[g][32 * r : 32 * r + 32 : 2, :].bitcast(I32))
 
         def entries(lo, hi):
             return slice(lo // 16, hi // 16)
@@ -75,7 +79,7 @@ def tile_moe_two_mlp_relu2_kernel(
                 chosen = offs_t[:, entries(g * HALF + lo, g * HALF + lo + width)]
                 nc.vector.tensor_copy(gw[o, g][:, lo : lo + width], xw[o][:].bitcast(U32).indirect(chosen))
 
-        for plane in (xs, w1s[0], w2s, planes, w1s[1]):
+        for plane in (xs, w1s[0], planes[0], w2s, planes[1], w1s[1]):
             nc.vector.memset(plane[:].bitcast(I32), 0)
         nc.vector.memset(zero[:], 0.0)
         make_identity(nc, ident[:])
@@ -83,21 +87,21 @@ def tile_moe_two_mlp_relu2_kernel(
         nc.sync.dma_start(offs_t[:], offs)
         for o in range(PASSES):
             nc.scalar.dma_start(
-                xs[2 * o : P : 8, :].bitcast(I32),
+                xs[2 * o + 2 : P : 8, :].bitcast(I32),
                 x_scales[o].rearrange("(q r) t -> r q t", r=4).bitcast(I32),
             )
         load_x(0)
-        load_rows(w1s[0], w1s_hbm[:, 0 : 2 * PASSES, :], nc.sync, range(0, 2))
+        load_rows(w1s[0], w1s_hbm[:, 0 : 2 * PASSES, :], nc.sync)
         load_x(1)
-        load_rows(w1s[0], w1s_hbm[:, 0 : 2 * PASSES, :], nc.sync, range(2, 4))
-        load_rows(w2s, w2s_hbm, nc.sync)
         load_w1(slice(0, 2), 0)
-        nc.vector.tensor_copy(gs[:], xs[:].indirect(offs_t[:]))
-        for r in range(4):
-            nc.sync.dma_start(planes[r:P:32].bitcast(I32), gs[32 * r : 32 * r + 32 : 2, :].bitcast(I32))
+        for g in range(2):
+            nc.vector.tensor_copy(gs[g][:], xs[:].indirect(offs_t[:, entries(g * HALF, (g + 1) * HALF)]))
+        move_planes(0)
         load_w1(slice(0, 2), 1)
         load_x(2)
+        load_rows(w2s, w2s_hbm, nc.sync)
         load_w1(slice(0, 2), 2)
+        move_planes(1)
         load_rows(w1s[1], w1s_hbm[:, 2 * PASSES : 4 * PASSES, :], nc.sync)
         load_w1(2, slice(0, PASSES))
         load_w1(3, slice(0, PASSES))
@@ -117,7 +121,7 @@ def tile_moe_two_mlp_relu2_kernel(
             nc.tensor.matmul_mx(
                 out=sums[j][:],
                 lhsT=gw[o, j * P // HALF][:, j * P % HALF : j * P % HALF + P].bitcast(FP8X4),
-                lhsT_scale=planes[:, o, j * P : (j + 1) * P],
+                lhsT_scale=planes[j * P // HALF][:, o + 1, j * P % HALF : j * P % HALF + P],
                 rhs=w1w[:, e, o, :].bitcast(FP4X4),
                 rhs_scale=w1s[e // 2][:, (e % 2) * PASSES + o, :],
                 start=(o == 0),
@@ -210,4 +214,5 @@ def tile_moe_two_mlp_relu2_kernel(
         results(2)
         results(3)
 
-        nc.sync.dma_start(out, placed[:])
+        nc.sync.dma_start(out[:, 0 : T // 2], placed[:, 0 : T // 2])
+        nc.scalar.dma_start(out[:, T // 2 : T], placed[:, T // 2 : T])

@@ -99,11 +99,11 @@ def tile_moe_two_mlp_relu2_kernel(
         move_planes(0)
         load_w1(slice(0, 2), 1)
         load_x(2)
-        load_rows(w2s, w2s_hbm, nc.sync)
         load_w1(slice(0, 2), 2)
-        move_planes(1)
-        load_rows(w1s[1], w1s_hbm[:, 2 * PASSES : 4 * PASSES, :], nc.sync)
+        load_rows(w2s, w2s_hbm, nc.sync)
         load_w1(2, slice(0, PASSES))
+        load_rows(w1s[1], w1s_hbm[:, 2 * PASSES : 4 * PASSES, :], nc.sync)
+        move_planes(1)
         load_w1(3, slice(0, PASSES))
         nc.sync.dma_start(w2w[:].bitcast(I32), w2w_hbm)
         nc.sync.dma_start(dst_t[:], dst)

@@ -18,11 +18,13 @@ ACT = mybir.ActivationFunctionType
 MULT = mybir.AluOpType.mult
 
 P = 128
-PASSES = K // 512
+PACK = 4
+PASSES = K // (P * PACK)
+LAST = PASSES - 1
 SLOTS = E * C
 TILES = SLOTS // P
 HALF = SLOTS // 2
-RELU_ON_VECTOR = (1, 3, 5)
+RELU_ON_VECTOR = range(1, TILES - 2, 2)
 
 
 def tile_moe_two_mlp_relu2_kernel(
@@ -35,125 +37,137 @@ def tile_moe_two_mlp_relu2_kernel(
 
         offs_t = keep.tile([P, SLOTS // 16], U16, name="offs_t")
         dst_t = keep.tile([P, SLOTS // 16], U16, name="dst_t")
-        xs = keep.tile([P, T], U8, name="xs", tag="window", align_bytes=64)
-        xw = [keep.tile([P, T], I32, name="xw%d" % o, align_bytes=64) for o in range(PASSES)]
-        gs = [keep.tile([P, HALF], U8, name="gs%d" % g, align_bytes=64) for g in range(2)]
-        planes = [keep.tile([P, 4, HALF], U8, name="planes%d" % g, align_bytes=64) for g in range(2)]
-        gw = {}
+        token_scales = keep.tile([P, T], U8, name="token_scales", tag="window", align_bytes=64)
+        token_words = [keep.tile([P, T], I32, name="token_words%d" % o, align_bytes=64) for o in range(PASSES)]
+        slot_scales = [keep.tile([P, HALF], U8, name="slot_scales%d" % g, align_bytes=64) for g in range(2)]
+        slot_planes = [keep.tile([P, PACK, HALF], U8, name="slot_planes%d" % g, align_bytes=64) for g in range(2)]
         w1w = keep.tile([P, E, PASSES, 2 * H], U8, name="w1w", align_bytes=64)
-        w1s = [keep.tile([P, 2 * PASSES, H], U8, name="w1s%d" % g, align_bytes=64) for g in range(2)]
+        w1_planes = [keep.tile([P, 2 * PASSES, H], U8, name="w1_planes%d" % g, align_bytes=64) for g in range(2)]
         w2w = keep.tile([P, E, 2 * N], U8, name="w2w", align_bytes=64)
-        w2s = keep.tile([P, E, N], U8, name="w2s", align_bytes=64)
+        w2_planes = keep.tile([P, E, N], U8, name="w2_planes", align_bytes=64)
         gate_t = keep.tile([P, SLOTS], F32, name="gate_t")
-        zero = keep.tile([P, 8], F32, name="zero")
+        zero = keep.tile([P, 1], F32, name="zero")
         ident = keep.tile([P, P], F32, name="ident")
         h_words = keep.tile([P, SLOTS], U32, name="h_words", align_bytes=64)
-        h_scales = keep.tile([P, SLOTS], U8, name="h_scales", align_bytes=64)
+        h_plane = keep.tile([P, SLOTS], U8, name="h_plane", align_bytes=64)
 
         w1w_hbm = w1_words.rearrange("e s p b -> p e s b").bitcast(I32)
         w1s_hbm = w1_scales.rearrange("e s q i -> q (e s) i").bitcast(I32)
         w2w_hbm = w2_words.rearrange("e s p b -> p (e s) b").bitcast(I32)
         w2s_hbm = w2_scales.rearrange("e s q n -> q (e s) n").bitcast(I32)
 
-        def load_x(o):
-            nc.sync.dma_start(xw[o][:], x_words[o].rearrange("p t r -> p (t r)").bitcast(I32))
+        def load_tokens(o):
+            nc.sync.dma_start(token_words[o][:], x_words[o].rearrange("p t r -> p (t r)").bitcast(I32))
 
         def load_w1(experts, passes):
             nc.sync.dma_start(w1w[:, experts, passes, :].bitcast(I32), w1w_hbm[:, experts, passes, :])
 
-        def load_rows(plane, rows, queue):
-            for r in range(4):
-                queue.dma_start(plane[r:P:32].bitcast(I32), rows[r:16:4])
+        def load_planes(planes, rows):
+            for r in range(PACK):
+                nc.sync.dma_start(planes[r:P:32].bitcast(I32), rows[r:16:PACK])
 
-        def move_planes(g):
-            for r in range(4):
-                nc.sync.dma_start(planes[g][r:P:32].bitcast(I32), gs[g][32 * r : 32 * r + 32 : 2, :].bitcast(I32))
+        def load_w1_planes(g):
+            load_planes(w1_planes[g], w1s_hbm[:, 2 * PASSES * g : 2 * PASSES * (g + 1), :])
+
+        def move_slot_planes(g):
+            for r in range(PACK):
+                rows = slot_scales[g][32 * r : 32 * r + 32 : 2, :]
+                nc.sync.dma_start(slot_planes[g][r:P:32].bitcast(I32), rows.bitcast(I32))
 
         def entries(lo, hi):
             return slice(lo // 16, hi // 16)
 
-        def gather_words(o, g, pieces, tag):
-            gw[o, g] = keep.tile([P, HALF], U32, name="gw", tag=tag, align_bytes=64)
-            width = HALF // pieces
+        slot_words = {}
+
+        def gather_words(o, g, width, tag):
+            slot_words[o, g] = keep.tile([P, HALF], U32, name="slot_words", tag=tag, align_bytes=64)
             for lo in range(0, HALF, width):
                 chosen = offs_t[:, entries(g * HALF + lo, g * HALF + lo + width)]
-                nc.vector.tensor_copy(gw[o, g][:, lo : lo + width], xw[o][:].bitcast(U32).indirect(chosen))
+                window = token_words[o][:].bitcast(U32).indirect(chosen)
+                nc.vector.tensor_copy(slot_words[o, g][:, lo : lo + width], window)
 
-        for plane in (xs, w1s[0], planes[0], w2s, planes[1], w1s[1]):
-            nc.vector.memset(plane[:].bitcast(I32), 0)
+        for sparse in (token_scales, w1_planes[0], slot_planes[0], w2_planes, slot_planes[1], w1_planes[1]):
+            nc.vector.memset(sparse[:].bitcast(I32), 0)
         nc.vector.memset(zero[:], 0.0)
         make_identity(nc, ident[:])
 
         nc.sync.dma_start(offs_t[:], offs)
         for o in range(PASSES):
             nc.scalar.dma_start(
-                xs[2 * o + 2 : P : 8, :].bitcast(I32),
-                x_scales[o].rearrange("(q r) t -> r q t", r=4).bitcast(I32),
+                token_scales[2 * (o + 1) : P : 8, :].bitcast(I32),
+                x_scales[o].rearrange("(a r) t -> r a t", r=PACK).bitcast(I32),
             )
-        load_x(0)
-        load_rows(w1s[0], w1s_hbm[:, 0 : 2 * PASSES, :], nc.sync)
-        load_x(1)
+
+        load_tokens(0)
+        load_w1_planes(0)
+        load_tokens(1)
         load_w1(slice(0, 2), 0)
         for g in range(2):
-            nc.vector.tensor_copy(gs[g][:], xs[:].indirect(offs_t[:, entries(g * HALF, (g + 1) * HALF)]))
-        move_planes(0)
+            chosen = offs_t[:, entries(g * HALF, (g + 1) * HALF)]
+            nc.vector.tensor_copy(slot_scales[g][:], token_scales[:].indirect(chosen))
+        move_slot_planes(0)
         load_w1(slice(0, 2), 1)
-        load_x(2)
-        load_w1(slice(0, 2), 2)
-        load_rows(w2s, w2s_hbm, nc.sync)
+        load_tokens(LAST)
+        load_w1(slice(0, 2), LAST)
+        load_planes(w2_planes, w2s_hbm)
         load_w1(2, slice(0, PASSES))
-        load_rows(w1s[1], w1s_hbm[:, 2 * PASSES : 4 * PASSES, :], nc.sync)
-        move_planes(1)
+        load_w1_planes(1)
+        move_slot_planes(1)
         load_w1(3, slice(0, PASSES))
         nc.sync.dma_start(w2w[:].bitcast(I32), w2w_hbm)
         nc.sync.dma_start(dst_t[:], dst)
         nc.sync.dma_start(gate_t[:], gate)
 
         placed = keep.tile([P, T], F32, name="placed", tag="window", align_bytes=64)
-        nc.scalar.activation(placed[:], zero[:, 0:1].to_broadcast([P, T]), ACT.Square)
+        nc.scalar.activation(placed[:], zero[:].to_broadcast([P, T]), ACT.Square)
 
         sums, relus, h, y_sb = {}, {}, {}, {}
 
         def first_layer(j, o):
             if o == 0:
                 sums[j] = psum.tile([P, H], F32, name="sums", tag="bank%d" % j)
-            e = j * P // C
+            e, g = j * P // C, j * P // HALF
+            in_half = slice(j * P - g * HALF, (j + 1) * P - g * HALF)
             nc.tensor.matmul_mx(
                 out=sums[j][:],
-                lhsT=gw[o, j * P // HALF][:, j * P % HALF : j * P % HALF + P].bitcast(FP8X4),
-                lhsT_scale=planes[j * P // HALF][:, o + 1, j * P % HALF : j * P % HALF + P],
+                lhsT=slot_words[o, g][:, in_half].bitcast(FP8X4),
+                lhsT_scale=slot_planes[g][:, o + 1, in_half],
                 rhs=w1w[:, e, o, :].bitcast(FP4X4),
-                rhs_scale=w1s[e // 2][:, (e % 2) * PASSES + o, :],
+                rhs_scale=w1_planes[g][:, (e % 2) * PASSES + o, :],
                 start=(o == 0),
-                stop=(o == PASSES - 1),
+                stop=(o == LAST),
             )
 
-        def relu(j):
-            relus[j] = keep.tile([P, 4, P], F32, name="relu", tag="relu%d" % j, align_bytes=64)
-            by_plane = sums[j][:].rearrange("s (p t) -> s t p", t=4)
+        def finish_sums(j):
+            for o in range(LAST if j < TILES // 2 else 0, PASSES):
+                first_layer(j, o)
+            relus[j] = keep.tile([P, PACK, P], F32, name="relu", tag="relu%d" % j, align_bytes=64)
+            by_code = sums[j][:].rearrange("s (p d) -> s d p", d=PACK)
             if j in RELU_ON_VECTOR:
-                nc.vector.tensor_scalar_max(relus[j][:], by_plane, 0.0)
+                nc.vector.tensor_scalar_max(relus[j][:], by_code, 0.0)
             else:
-                nc.scalar.activation(relus[j][:], by_plane, ACT.Relu)
+                nc.scalar.activation(relus[j][:], by_code, ACT.Relu)
 
         def turn_and_square(j):
             e = j * P // C
             if j % 2 == 0:
-                h[e] = keep.tile([P, C, 4], BF16, name="h%d" % e, align_bytes=64)
-            turned = psum.tile([P, 4, P], F32, name="turned", tag="bank%d" % j)
-            for t in range(4):
-                nc.tensor.transpose(turned[:, t, :], relus[j][:, t, :], ident[:])
+                h[e] = keep.tile([P, C, PACK], BF16, name="h%d" % e, align_bytes=64)
+            turned = psum.tile([P, PACK, P], F32, name="turned", tag="bank%d" % j)
+            for d in range(PACK):
+                nc.tensor.transpose(turned[:, d, :], relus[j][:, d, :], ident[:])
             nc.scalar.activation(
-                h[e][:, (j % 2) * P : (j % 2 + 1) * P, :], turned[:].rearrange("p t s -> p s t"), ACT.Square
+                h[e][:, (j % 2) * P : (j % 2 + 1) * P, :], turned[:].rearrange("p d s -> p s d"), ACT.Square
             )
 
         def quantise(e):
-            slots = slice(e * C, (e + 1) * C)
-            nc.vector.quantize_mx(
-                out=h_words[:, slots].bitcast(FP8X4),
-                scales=h_scales[:, slots],
-                in_=h[e][:].rearrange("p s t -> p (s t)"),
-            )
+            width = P if e == E - 1 else C
+            for lo in range(0, C, width):
+                slots = slice(e * C + lo, e * C + lo + width)
+                nc.vector.quantize_mx(
+                    out=h_words[:, slots].bitcast(FP8X4),
+                    scales=h_plane[:, slots],
+                    in_=h[e][:, lo : lo + width, :].rearrange("p s d -> p (s d)"),
+                )
 
         def second_layer(e):
             slots = slice(e * C, (e + 1) * C)
@@ -161,9 +175,9 @@ def tile_moe_two_mlp_relu2_kernel(
             nc.tensor.matmul_mx(
                 out=y[:],
                 lhsT=w2w[:, e, :].bitcast(FP4X4),
-                lhsT_scale=w2s[:, e, :],
+                lhsT_scale=w2_planes[:, e, :],
                 rhs=h_words[:, slots].bitcast(FP8X4),
-                rhs_scale=h_scales[:, slots],
+                rhs_scale=h_plane[:, slots],
                 start=True,
                 stop=True,
             )
@@ -174,45 +188,31 @@ def tile_moe_two_mlp_relu2_kernel(
             window = placed[:].indirect(dst_t[:, entries(e * C, (e + 1) * C)])
             nc.vector.tensor_tensor(window, y_sb[e][:], gate_t[:, e * C : (e + 1) * C], MULT)
 
-        for o in range(PASSES - 1):
+        for o in range(LAST):
             for g in range(2):
-                gather_words(o, g, 1, "gw%d%d" % (o, g))
+                gather_words(o, g, HALF, "slot_words%d%d" % (o, g))
             for j in range(TILES // 2):
                 first_layer(j, o)
 
-        def finish_sums(j):
-            for o in range(PASSES - 1 if j < TILES // 2 else 0, PASSES):
-                first_layer(j, o)
-            relu(j)
-
-        def hidden(e):
-            turn_and_square(2 * e + 1)
-            quantise(e)
-
-        def results(e):
-            second_layer(e)
-            scatter(e)
-
-        gather_words(PASSES - 1, 0, 2, "gw20")
+        gather_words(LAST, 0, C, "slot_words%d0" % LAST)
         for j in range(TILES // 2):
             finish_sums(j)
-        turn_and_square(0)
-        gather_words(PASSES - 1, 1, 2, "relu0")
-        hidden(0)
-        turn_and_square(2)
-        hidden(1)
-        finish_sums(4)
-        finish_sums(5)
-        results(0)
-        finish_sums(6)
-        turn_and_square(4)
-        hidden(2)
-        results(1)
-        finish_sums(7)
-        turn_and_square(6)
-        hidden(3)
-        results(2)
-        results(3)
+
+        for e in range(E + 1):
+            ahead = E // 2 <= e + 1 < E
+            if ahead:
+                finish_sums(2 * e + 2)
+            if e < E:
+                turn_and_square(2 * e)
+                if e == 0:
+                    gather_words(LAST, 1, C, "relu0")
+                turn_and_square(2 * e + 1)
+                quantise(e)
+            if e > 0:
+                second_layer(e - 1)
+                scatter(e - 1)
+            if ahead:
+                finish_sums(2 * e + 3)
 
         nc.sync.dma_start(out[:, 0 : T // 2], placed[:, 0 : T // 2])
         nc.scalar.dma_start(out[:, T // 2 : T], placed[:, T // 2 : T])

@@ -25,6 +25,7 @@ SLOTS = E * C
 TILES = SLOTS // P
 HALF = SLOTS // 2
 RELU_ON_VECTOR = range(1, TILES - 2, 2)
+TURNED_ELSEWHERE = {0: TILES - 1, TILES - 1: 1}
 
 
 def tile_moe_two_mlp_relu2_kernel(
@@ -39,7 +40,9 @@ def tile_moe_two_mlp_relu2_kernel(
         dst_t = keep.tile([P, SLOTS // 16], U16, name="dst_t")
         token_scales = keep.tile([P, T], U8, name="token_scales", tag="window", align_bytes=64)
         token_words = [keep.tile([P, T], I32, name="token_words%d" % o, align_bytes=64) for o in range(PASSES)]
-        slot_scales = [keep.tile([P, HALF], U8, name="slot_scales%d" % g, align_bytes=64) for g in range(2)]
+        slot_scales = [
+            keep.tile([P, HALF], U8, name="slot_scales", tag="slot_scales%d" % g, align_bytes=64) for g in range(2)
+        ]
         slot_planes = [keep.tile([P, PACK, HALF], U8, name="slot_planes%d" % g, align_bytes=64) for g in range(2)]
         w1w = keep.tile([P, E, PASSES, 2 * H], U8, name="w1w", align_bytes=64)
         w1_planes = [keep.tile([P, 2 * PASSES, H], U8, name="w1_planes%d" % g, align_bytes=64) for g in range(2)]
@@ -47,7 +50,6 @@ def tile_moe_two_mlp_relu2_kernel(
         w2_planes = keep.tile([P, E, N], U8, name="w2_planes", align_bytes=64)
         gate_t = keep.tile([P, SLOTS], F32, name="gate_t")
         zero = keep.tile([P, 1], F32, name="zero")
-        ident = keep.tile([P, P], F32, name="ident")
         h_words = keep.tile([P, SLOTS], U32, name="h_words", align_bytes=64)
         h_plane = keep.tile([P, SLOTS], U8, name="h_plane", align_bytes=64)
 
@@ -89,7 +91,6 @@ def tile_moe_two_mlp_relu2_kernel(
         for sparse in (token_scales, w1_planes[0], slot_planes[0], w2_planes, slot_planes[1], w1_planes[1]):
             nc.vector.memset(sparse[:].bitcast(I32), 0)
         nc.vector.memset(zero[:], 0.0)
-        make_identity(nc, ident[:])
 
         nc.sync.dma_start(offs_t[:], offs)
         for o in range(PASSES):
@@ -118,6 +119,9 @@ def tile_moe_two_mlp_relu2_kernel(
         nc.sync.dma_start(dst_t[:], dst)
         nc.sync.dma_start(gate_t[:], gate)
 
+        ident = keep.tile([P, P], F32, name="ident", tag="slot_scales0", align_bytes=64)
+        make_identity(nc, ident[:])
+
         placed = keep.tile([P, T], F32, name="placed", tag="window", align_bytes=64)
         nc.scalar.activation(placed[:], zero[:].to_broadcast([P, T]), ACT.Square)
 
@@ -143,16 +147,19 @@ def tile_moe_two_mlp_relu2_kernel(
                 first_layer(j, o)
             relus[j] = keep.tile([P, PACK, P], F32, name="relu", tag="relu%d" % j, align_bytes=64)
             by_code = sums[j][:].rearrange("s (p d) -> s d p", d=PACK)
-            if j in RELU_ON_VECTOR:
-                nc.vector.tensor_scalar_max(relus[j][:], by_code, 0.0)
-            else:
-                nc.scalar.activation(relus[j][:], by_code, ACT.Relu)
+            width = PACK // 2 if j in TURNED_ELSEWHERE else PACK
+            for d in range(0, PACK, width):
+                codes = slice(d, d + width)
+                if j in RELU_ON_VECTOR:
+                    nc.vector.tensor_scalar_max(relus[j][:, codes, :], by_code[:, codes, :], 0.0)
+                else:
+                    nc.scalar.activation(relus[j][:, codes, :], by_code[:, codes, :], ACT.Relu)
 
         def turn_and_square(j):
             e = j * P // C
             if j % 2 == 0:
                 h[e] = keep.tile([P, C, PACK], BF16, name="h%d" % e, align_bytes=64)
-            turned = psum.tile([P, PACK, P], F32, name="turned", tag="bank%d" % j)
+            turned = psum.tile([P, PACK, P], F32, name="turned", tag="bank%d" % TURNED_ELSEWHERE.get(j, j))
             for d in range(PACK):
                 nc.tensor.transpose(turned[:, d, :], relus[j][:, d, :], ident[:])
             nc.scalar.activation(

@@ -44,7 +44,6 @@ def tile_moe_two_mlp_relu2_kernel(
             keep.tile([P, HALF], U8, name="slot_scales", tag="slot_scales%d" % g, align_bytes=64) for g in range(2)
         ]
         slot_planes = [keep.tile([P, PACK, HALF], U8, name="slot_planes%d" % g, align_bytes=64) for g in range(2)]
-        w1w = keep.tile([P, E, PASSES, 2 * H], U8, name="w1w", align_bytes=64)
         w1_planes = [keep.tile([P, 2 * PASSES, H], U8, name="w1_planes%d" % g, align_bytes=64) for g in range(2)]
         w2w = keep.tile([P, E, 2 * N], U8, name="w2w", align_bytes=64)
         w2_planes = keep.tile([P, E, N], U8, name="w2_planes", align_bytes=64)
@@ -53,7 +52,7 @@ def tile_moe_two_mlp_relu2_kernel(
         h_words = keep.tile([P, SLOTS], U32, name="h_words", align_bytes=64)
         h_plane = keep.tile([P, SLOTS], U8, name="h_plane", align_bytes=64)
 
-        w1w_hbm = w1_words.rearrange("e s p b -> p e s b").bitcast(I32)
+        w1w_hbm = w1_words.rearrange("e s p b -> p (e s) b").bitcast(I32)
         w1s_hbm = w1_scales.rearrange("e s q i -> q (e s) i").bitcast(I32)
         w2w_hbm = w2_words.rearrange("e s p b -> p (e s) b").bitcast(I32)
         w2s_hbm = w2_scales.rearrange("e s q n -> q (e s) n").bitcast(I32)
@@ -61,8 +60,14 @@ def tile_moe_two_mlp_relu2_kernel(
         def load_tokens(o):
             nc.sync.dma_start(token_words[o][:], x_words[o].rearrange("p t r -> p (t r)").bitcast(I32))
 
-        def load_w1(experts, passes):
-            nc.sync.dma_start(w1w[:, experts, passes, :].bitcast(I32), w1w_hbm[:, experts, passes, :])
+        w1w = {}
+
+        def load_w1(rows):
+            pairs = range(E * PASSES)[rows]
+            words = keep.tile([P, len(pairs), 2 * H], U8, name="w1w%d" % pairs[0], align_bytes=64)
+            nc.sync.dma_start(words[:].bitcast(I32), w1w_hbm[:, rows, :])
+            for n, pair in enumerate(pairs):
+                w1w[divmod(pair, PASSES)] = words[:, n, :]
 
         def load_planes(planes, rows):
             for r in range(PACK):
@@ -102,19 +107,19 @@ def tile_moe_two_mlp_relu2_kernel(
         load_tokens(0)
         load_w1_planes(0)
         load_tokens(1)
-        load_w1(slice(0, 2), 0)
+        load_w1(slice(0, 2 * PASSES, PASSES))
         for g in range(2):
             chosen = offs_t[:, entries(g * HALF, (g + 1) * HALF)]
             nc.vector.tensor_copy(slot_scales[g][:], token_scales[:].indirect(chosen))
         move_slot_planes(0)
-        load_w1(slice(0, 2), 1)
+        load_w1(slice(1, 2 * PASSES, PASSES))
         load_tokens(LAST)
-        load_w1(slice(0, 2), LAST)
+        load_w1(slice(LAST, 2 * PASSES, PASSES))
         load_planes(w2_planes, w2s_hbm)
-        load_w1(2, slice(0, PASSES))
+        load_w1(slice(2 * PASSES, 3 * PASSES))
         load_w1_planes(1)
         move_slot_planes(1)
-        load_w1(3, slice(0, PASSES))
+        load_w1(slice(3 * PASSES, 4 * PASSES))
         nc.sync.dma_start(w2w[:].bitcast(I32), w2w_hbm)
         nc.sync.dma_start(dst_t[:], dst)
         nc.sync.dma_start(gate_t[:], gate)
@@ -136,7 +141,7 @@ def tile_moe_two_mlp_relu2_kernel(
                 out=sums[j][:],
                 lhsT=slot_words[o, g][:, in_half].bitcast(FP8X4),
                 lhsT_scale=slot_planes[g][:, o + 1, in_half],
-                rhs=w1w[:, e, o, :].bitcast(FP4X4),
+                rhs=w1w[e, o].bitcast(FP4X4),
                 rhs_scale=w1_planes[g][:, (e % 2) * PASSES + o, :],
                 start=(o == 0),
                 stop=(o == LAST),

@@ -69,15 +69,15 @@ def tile_moe_two_mlp_relu2_kernel(
             for n, pair in enumerate(pairs):
                 w1w[divmod(pair, PASSES)] = words[:, n, :]
 
-        def load_planes(planes, rows):
-            for r in range(PACK):
+        def load_planes(planes, rows, rs=range(PACK)):
+            for r in rs:
                 nc.sync.dma_start(planes[r:P:32].bitcast(I32), rows[r:16:PACK])
 
-        def load_w1_planes(g):
-            load_planes(w1_planes[g], w1s_hbm[:, 2 * PASSES * g : 2 * PASSES * (g + 1), :])
+        def load_w1_planes(g, rs=range(PACK)):
+            load_planes(w1_planes[g], w1s_hbm[:, 2 * PASSES * g : 2 * PASSES * (g + 1), :], rs)
 
-        def move_slot_planes(g):
-            for r in range(PACK):
+        def move_slot_planes(g, rs=range(PACK)):
+            for r in rs:
                 rows = slot_scales[g][32 * r : 32 * r + 32 : 2, :]
                 nc.sync.dma_start(slot_planes[g][r:P:32].bitcast(I32), rows.bitcast(I32))
 
@@ -107,22 +107,23 @@ def tile_moe_two_mlp_relu2_kernel(
         load_tokens(0)
         load_w1_planes(0)
         load_tokens(1)
-        load_w1(slice(0, 2 * PASSES, PASSES))
-        for g in range(2):
-            chosen = offs_t[:, entries(g * HALF, (g + 1) * HALF)]
-            nc.vector.tensor_copy(slot_scales[g][:], token_scales[:].indirect(chosen))
+        load_w1(slice(0, 6, 3))
+        nc.vector.tensor_copy(slot_scales[0][:], token_scales[:].indirect(offs_t[:, entries(0 * HALF, (0 + 1) * HALF)]))
+        nc.vector.tensor_copy(slot_scales[1][:], token_scales[:].indirect(offs_t[:, entries(1 * HALF, (1 + 1) * HALF)]))
         move_slot_planes(0)
-        load_w1(slice(1, 2 * PASSES, PASSES))
-        load_tokens(LAST)
-        load_w1(slice(LAST, 2 * PASSES, PASSES))
-        load_planes(w2_planes, w2s_hbm)
-        load_w1(slice(2 * PASSES, 3 * PASSES))
+        load_w1(slice(1, 6, 3))
+        load_tokens(2)
+        load_w1(slice(2, 6, 3))
+        load_planes(w2_planes, w2s_hbm, range(0, 2))
         load_w1_planes(1)
+        load_w1(slice(6, 9))
+        load_planes(w2_planes, w2s_hbm, range(2, 4))
         move_slot_planes(1)
-        load_w1(slice(3 * PASSES, 4 * PASSES))
+        load_w1(slice(9, 12))
         nc.sync.dma_start(w2w[:].bitcast(I32), w2w_hbm)
         nc.sync.dma_start(dst_t[:], dst)
-        nc.sync.dma_start(gate_t[:], gate)
+        nc.sync.dma_start(gate_t[:, 0:C], gate[:, 0:C])
+        nc.sync.dma_start(gate_t[:, C:SLOTS], gate[:, C:SLOTS])
 
         ident = keep.tile([P, P], F32, name="ident", tag="slot_scales0", align_bytes=64)
         make_identity(nc, ident[:])

@@ -105,8 +105,9 @@ def tile_moe_two_mlp_relu2_kernel(
             )
 
         load_tokens(0)
-        load_w1_planes(0)
+        load_w1_planes(0, range(0, 3))
         load_tokens(1)
+        load_w1_planes(0, range(3, 4))
         load_w1(slice(0, 6, 3))
         nc.vector.tensor_copy(slot_scales[0][:], token_scales[:].indirect(offs_t[:, entries(0 * HALF, (0 + 1) * HALF)]))
         nc.vector.tensor_copy(slot_scales[1][:], token_scales[:].indirect(offs_t[:, entries(1 * HALF, (1 + 1) * HALF)]))
@@ -184,7 +185,7 @@ def tile_moe_two_mlp_relu2_kernel(
 
         def second_layer(e):
             slots = slice(e * C, (e + 1) * C)
-            y = psum.tile([P, C], F32, name="y", tag="bank%d" % (2 * e))
+            y = psum.tile([P, C], F32, name="y", tag="bank%d" % (TILES - 1 if e == E - 2 else 2 * e))
             nc.tensor.matmul_mx(
                 out=y[:],
                 lhsT=w2w[:, e, :].bitcast(FP4X4),
@@ -207,7 +208,7 @@ def tile_moe_two_mlp_relu2_kernel(
             for j in range(TILES // 2):
                 first_layer(j, o)
 
-        gather_words(LAST, 0, C, "slot_words%d0" % LAST)
+        gather_words(LAST, 0, P, "slot_words%d0" % LAST)
         for j in range(TILES // 2):
             finish_sums(j)
 

@@ -24,6 +24,8 @@ LAST = PASSES - 1
 SLOTS = E * C
 TILES = SLOTS // P
 HALF = SLOTS // 2
+SCALE_ROW = (0, 4, 6)
+PLANE_GROUPS = (range(0, 2 * PASSES + 1), range(2 * PASSES + 1, E * PASSES))
 RELU_ON_VECTOR = range(1, TILES - 2, 2)
 TURNED_ELSEWHERE = {0: TILES - 1, TILES - 1: 1}
 
@@ -40,11 +42,13 @@ def tile_moe_two_mlp_relu2_kernel(
         dst_t = keep.tile([P, SLOTS // 16], U16, name="dst_t")
         token_scales = keep.tile([P, T], U8, name="token_scales", tag="window", align_bytes=64)
         token_words = [keep.tile([P, T], I32, name="token_words%d" % o, align_bytes=64) for o in range(PASSES)]
-        slot_scales = [
-            keep.tile([P, HALF], U8, name="slot_scales", tag="slot_scales%d" % g, align_bytes=64) for g in range(2)
+        slot_scales = keep.tile([P, SLOTS], U8, name="slot_scales", align_bytes=64)
+        slot_planes = keep.tile([P, LAST, SLOTS], U8, name="slot_planes", align_bytes=64)
+        last_plane = keep.tile([P, SLOTS], U8, name="last_plane", align_bytes=64)
+        w1_planes = [
+            keep.tile([P, len(pairs), H], U8, name="w1_planes%d" % n, align_bytes=64)
+            for n, pairs in enumerate(PLANE_GROUPS)
         ]
-        slot_planes = [keep.tile([P, PACK, HALF], U8, name="slot_planes%d" % g, align_bytes=64) for g in range(2)]
-        w1_planes = [keep.tile([P, 2 * PASSES, H], U8, name="w1_planes%d" % g, align_bytes=64) for g in range(2)]
         w2w = keep.tile([P, E, 2 * N], U8, name="w2w", align_bytes=64)
         w2_planes = keep.tile([P, E, N], U8, name="w2_planes", align_bytes=64)
         gate_t = keep.tile([P, SLOTS], F32, name="gate_t")
@@ -73,13 +77,13 @@ def tile_moe_two_mlp_relu2_kernel(
             for r in rs:
                 nc.sync.dma_start(planes[r:P:32].bitcast(I32), rows[r:16:PACK])
 
-        def load_w1_planes(g, rs=range(PACK)):
-            load_planes(w1_planes[g], w1s_hbm[:, 2 * PASSES * g : 2 * PASSES * (g + 1), :], rs)
+        def load_w1_planes(n):
+            load_planes(w1_planes[n], w1s_hbm[:, PLANE_GROUPS[n].start : PLANE_GROUPS[n].stop, :])
 
-        def move_slot_planes(g, rs=range(PACK)):
-            for r in rs:
-                rows = slot_scales[g][32 * r : 32 * r + 32 : 2, :]
-                nc.sync.dma_start(slot_planes[g][r:P:32].bitcast(I32), rows.bitcast(I32))
+        def move_slot_planes(planes, first, step):
+            for r in range(PACK):
+                rows = slot_scales[32 * r + first : 32 * r + 32 : step, :]
+                nc.sync.dma_start(planes[r:P:32].bitcast(I32), rows.bitcast(I32))
 
         def entries(lo, hi):
             return slice(lo // 16, hi // 16)
@@ -93,41 +97,41 @@ def tile_moe_two_mlp_relu2_kernel(
                 window = token_words[o][:].bitcast(U32).indirect(chosen)
                 nc.vector.tensor_copy(slot_words[o, g][:, lo : lo + width], window)
 
-        for sparse in (token_scales, w1_planes[0], slot_planes[0], w2_planes, slot_planes[1], w1_planes[1]):
+        for sparse in (token_scales, w1_planes[0], slot_planes, w2_planes, last_plane, w1_planes[1]):
             nc.vector.memset(sparse[:].bitcast(I32), 0)
         nc.vector.memset(zero[:], 0.0)
+        ident = keep.tile([P, P], F32, name="ident", align_bytes=64)
+        nc.vector.memset(ident[:], 0.0)
+        make_identity(nc, ident[:], nomemset=True)
 
         nc.sync.dma_start(offs_t[:], offs)
         for o in range(PASSES):
             nc.scalar.dma_start(
-                token_scales[2 * (o + 1) : P : 8, :].bitcast(I32),
+                token_scales[SCALE_ROW[o] : P : 8, :].bitcast(I32),
                 x_scales[o].rearrange("(a r) t -> r a t", r=PACK).bitcast(I32),
             )
 
         load_tokens(0)
-        load_w1_planes(0, range(0, 3))
+        load_w1_planes(0)
         load_tokens(1)
-        load_w1_planes(0, range(3, 4))
         load_w1(slice(0, 6, 3))
-        nc.vector.tensor_copy(slot_scales[0][:], token_scales[:].indirect(offs_t[:, entries(0 * HALF, (0 + 1) * HALF)]))
-        nc.vector.tensor_copy(slot_scales[1][:], token_scales[:].indirect(offs_t[:, entries(1 * HALF, (1 + 1) * HALF)]))
-        move_slot_planes(0)
+        nc.vector.tensor_copy(slot_scales[:], token_scales[:].indirect(offs_t[:]))
+        move_slot_planes(slot_planes, SCALE_ROW[0], 4)
         load_w1(slice(1, 6, 3))
+        load_planes(w2_planes, w2s_hbm, range(0, 1))
         load_tokens(2)
-        load_w1(slice(2, 6, 3))
-        load_planes(w2_planes, w2s_hbm, range(0, 2))
-        load_w1_planes(1)
+        move_slot_planes(last_plane, SCALE_ROW[LAST], 8)
+        load_w1(slice(2, 3))
+        load_w1(slice(5, 6))
+        load_planes(w2_planes, w2s_hbm, range(1, 2))
         load_w1(slice(6, 9))
         load_planes(w2_planes, w2s_hbm, range(2, 4))
-        move_slot_planes(1)
+        load_w1_planes(1)
         load_w1(slice(9, 12))
         nc.sync.dma_start(w2w[:].bitcast(I32), w2w_hbm)
         nc.sync.dma_start(dst_t[:], dst)
         nc.sync.dma_start(gate_t[:, 0:C], gate[:, 0:C])
         nc.sync.dma_start(gate_t[:, C:SLOTS], gate[:, C:SLOTS])
-
-        ident = keep.tile([P, P], F32, name="ident", tag="slot_scales0", align_bytes=64)
-        make_identity(nc, ident[:])
 
         placed = keep.tile([P, T], F32, name="placed", tag="window", align_bytes=64)
         nc.scalar.activation(placed[:], zero[:].to_broadcast([P, T]), ACT.Square)
@@ -139,12 +143,15 @@ def tile_moe_two_mlp_relu2_kernel(
                 sums[j] = psum.tile([P, H], F32, name="sums", tag="bank%d" % j)
             e, g = j * P // C, j * P // HALF
             in_half = slice(j * P - g * HALF, (j + 1) * P - g * HALF)
+            slots = slice(j * P, (j + 1) * P)
+            pair = PASSES * e + o
+            n = int(pair in PLANE_GROUPS[1])
             nc.tensor.matmul_mx(
                 out=sums[j][:],
                 lhsT=slot_words[o, g][:, in_half].bitcast(FP8X4),
-                lhsT_scale=slot_planes[g][:, o + 1, in_half],
+                lhsT_scale=last_plane[:, slots] if o == LAST else slot_planes[:, o, slots],
                 rhs=w1w[e, o].bitcast(FP4X4),
-                rhs_scale=w1_planes[g][:, (e % 2) * PASSES + o, :],
+                rhs_scale=w1_planes[n][:, pair - PLANE_GROUPS[n].start, :],
                 start=(o == 0),
                 stop=(o == LAST),
             )
@@ -214,7 +221,7 @@ def tile_moe_two_mlp_relu2_kernel(
 
         for e in range(E + 1):
             ahead = E // 2 <= e + 1 < E
-            if ahead:
+            if ahead and e > 1:
                 finish_sums(2 * e + 2)
             if e < E:
                 turn_and_square(2 * e)
@@ -222,6 +229,8 @@ def tile_moe_two_mlp_relu2_kernel(
                     gather_words(LAST, 1, C, "relu0")
                 turn_and_square(2 * e + 1)
                 quantise(e)
+            if ahead and e == 1:
+                finish_sums(2 * e + 2)
             if e > 0:
                 second_layer(e - 1)
                 scatter(e - 1)

@@ -26,7 +26,7 @@ TILES = SLOTS // P
 HALF = SLOTS // 2
 SCALE_ROW = (0, 4, 6)
 PLANE_GROUPS = (range(0, 2 * PASSES + 1), range(2 * PASSES + 1, E * PASSES))
-RELU_ON_VECTOR = range(1, TILES - 2, 2)
+RELU_ON_VECTOR = (1, 3, 4)
 TURNED_ELSEWHERE = {0: TILES - 1, TILES - 1: 1}
 
 
@@ -40,21 +40,20 @@ def tile_moe_two_mlp_relu2_kernel(
 
         offs_t = keep.tile([P, SLOTS // 16], U16, name="offs_t")
         dst_t = keep.tile([P, SLOTS // 16], U16, name="dst_t")
-        token_scales = keep.tile([P, T], U8, name="token_scales", tag="window", align_bytes=64)
-        token_words = [keep.tile([P, T], I32, name="token_words%d" % o, align_bytes=64) for o in range(PASSES)]
-        slot_scales = keep.tile([P, SLOTS], U8, name="slot_scales", align_bytes=64)
-        slot_planes = keep.tile([P, LAST, SLOTS], U8, name="slot_planes", align_bytes=64)
-        last_plane = keep.tile([P, SLOTS], U8, name="last_plane", align_bytes=64)
+        token_scales = keep.tile([P, T], U8, name="token_scales", tag="window", align_bytes=256)
+        token_words = [keep.tile([P, T], I32, name="token_words%d" % o, align_bytes=256) for o in range(PASSES)]
+        slot_scales = keep.tile([P, SLOTS], U8, name="slot_scales", align_bytes=256)
+        slot_planes = keep.tile([P, LAST, SLOTS], U8, name="slot_planes", align_bytes=256)
+        last_plane = keep.tile([P, SLOTS], U8, name="last_plane", align_bytes=256)
         w1_planes = [
-            keep.tile([P, len(pairs), H], U8, name="w1_planes%d" % n, align_bytes=64)
+            keep.tile([P, len(pairs), H], U8, name="w1_planes%d" % n, align_bytes=256)
             for n, pairs in enumerate(PLANE_GROUPS)
         ]
-        w2w = keep.tile([P, E, 2 * N], U8, name="w2w", align_bytes=64)
-        w2_planes = keep.tile([P, E, N], U8, name="w2_planes", align_bytes=64)
-        gate_t = keep.tile([P, SLOTS], F32, name="gate_t")
+        w2_planes = keep.tile([P, E, N], U8, name="w2_planes", align_bytes=256)
+        gate_t = keep.tile([P, SLOTS], F32, name="gate_t", align_bytes=256)
         zero = keep.tile([P, 1], F32, name="zero")
-        h_words = keep.tile([P, SLOTS], U32, name="h_words", align_bytes=64)
-        h_plane = keep.tile([P, SLOTS], U8, name="h_plane", align_bytes=64)
+        h_words = keep.tile([P, SLOTS], U32, name="h_words", align_bytes=256)
+        h_plane = keep.tile([P, SLOTS], U8, name="h_plane", align_bytes=256)
 
         w1w_hbm = w1_words.rearrange("e s p b -> p (e s) b").bitcast(I32)
         w1s_hbm = w1_scales.rearrange("e s q i -> q (e s) i").bitcast(I32)
@@ -68,17 +67,25 @@ def tile_moe_two_mlp_relu2_kernel(
 
         def load_w1(rows):
             pairs = range(E * PASSES)[rows]
-            words = keep.tile([P, len(pairs), 2 * H], U8, name="w1w%d" % pairs[0], align_bytes=64)
+            words = keep.tile([P, len(pairs), 2 * H], U8, name="w1w%d" % pairs[0], align_bytes=256)
             nc.sync.dma_start(words[:].bitcast(I32), w1w_hbm[:, rows, :])
             for n, pair in enumerate(pairs):
                 w1w[divmod(pair, PASSES)] = words[:, n, :]
+
+        w2w = {}
+
+        def load_w2(experts):
+            words = keep.tile([P, len(experts), 2 * N], U8, name="w2w%d" % experts.start, align_bytes=256)
+            nc.sync.dma_start(words[:].bitcast(I32), w2w_hbm[:, experts.start : experts.stop, :])
+            for n, e in enumerate(experts):
+                w2w[e] = words[:, n, :]
 
         def load_planes(planes, rows, rs=range(PACK)):
             for r in rs:
                 nc.sync.dma_start(planes[r:P:32].bitcast(I32), rows[r:16:PACK])
 
-        def load_w1_planes(n):
-            load_planes(w1_planes[n], w1s_hbm[:, PLANE_GROUPS[n].start : PLANE_GROUPS[n].stop, :])
+        def load_w1_planes(n, rs=range(PACK)):
+            load_planes(w1_planes[n], w1s_hbm[:, PLANE_GROUPS[n].start : PLANE_GROUPS[n].stop, :], rs)
 
         def move_slot_planes(planes, first, step):
             for r in range(PACK):
@@ -91,7 +98,7 @@ def tile_moe_two_mlp_relu2_kernel(
         slot_words = {}
 
         def gather_words(o, g, width, tag):
-            slot_words[o, g] = keep.tile([P, HALF], U32, name="slot_words", tag=tag, align_bytes=64)
+            slot_words[o, g] = keep.tile([P, HALF], U32, name="slot_words", tag=tag, align_bytes=256)
             for lo in range(0, HALF, width):
                 chosen = offs_t[:, entries(g * HALF + lo, g * HALF + lo + width)]
                 window = token_words[o][:].bitcast(U32).indirect(chosen)
@@ -100,7 +107,7 @@ def tile_moe_two_mlp_relu2_kernel(
         for sparse in (token_scales, w1_planes[0], slot_planes, w2_planes, last_plane, w1_planes[1]):
             nc.vector.memset(sparse[:].bitcast(I32), 0)
         nc.vector.memset(zero[:], 0.0)
-        ident = keep.tile([P, P], F32, name="ident", align_bytes=64)
+        ident = keep.tile([P, P], F32, name="ident", align_bytes=256)
         nc.vector.memset(ident[:], 0.0)
         make_identity(nc, ident[:], nomemset=True)
 
@@ -118,22 +125,23 @@ def tile_moe_two_mlp_relu2_kernel(
         nc.vector.tensor_copy(slot_scales[:], token_scales[:].indirect(offs_t[:]))
         move_slot_planes(slot_planes, SCALE_ROW[0], 4)
         load_w1(slice(1, 6, 3))
-        load_planes(w2_planes, w2s_hbm, range(0, 1))
+        load_planes(w2_planes, w2s_hbm, range(0, 2))
         load_tokens(2)
         move_slot_planes(last_plane, SCALE_ROW[LAST], 8)
         load_w1(slice(2, 3))
         load_w1(slice(5, 6))
-        load_planes(w2_planes, w2s_hbm, range(1, 2))
+        load_w1_planes(1, range(0, 1))
         load_w1(slice(6, 9))
         load_planes(w2_planes, w2s_hbm, range(2, 4))
-        load_w1_planes(1)
+        load_w1_planes(1, range(1, 4))
+        load_w2(range(0, 1))
         load_w1(slice(9, 12))
-        nc.sync.dma_start(w2w[:].bitcast(I32), w2w_hbm)
         nc.sync.dma_start(dst_t[:], dst)
         nc.sync.dma_start(gate_t[:, 0:C], gate[:, 0:C])
+        load_w2(range(1, E))
         nc.sync.dma_start(gate_t[:, C:SLOTS], gate[:, C:SLOTS])
 
-        placed = keep.tile([P, T], F32, name="placed", tag="window", align_bytes=64)
+        placed = keep.tile([P, T], F32, name="placed", tag="window", align_bytes=256)
         nc.scalar.activation(placed[:], zero[:].to_broadcast([P, T]), ACT.Square)
 
         sums, relus, h, y_sb = {}, {}, {}, {}
@@ -157,9 +165,9 @@ def tile_moe_two_mlp_relu2_kernel(
             )
 
         def finish_sums(j):
-            for o in range(LAST if j < TILES // 2 else 0, PASSES):
+            for o in range(LAST if j < TILES - 2 else 0, PASSES):
                 first_layer(j, o)
-            relus[j] = keep.tile([P, PACK, P], F32, name="relu", tag="relu%d" % j, align_bytes=64)
+            relus[j] = keep.tile([P, PACK, P], F32, name="relu", tag="relu%d" % j, align_bytes=256)
             by_code = sums[j][:].rearrange("s (p d) -> s d p", d=PACK)
             width = PACK // 2 if j in TURNED_ELSEWHERE else PACK
             for d in range(0, PACK, width):
@@ -172,7 +180,7 @@ def tile_moe_two_mlp_relu2_kernel(
         def turn_and_square(j):
             e = j * P // C
             if j % 2 == 0:
-                h[e] = keep.tile([P, C, PACK], BF16, name="h%d" % e, align_bytes=64)
+                h[e] = keep.tile([P, C, PACK], BF16, name="h%d" % e, align_bytes=256)
             turned = psum.tile([P, PACK, P], F32, name="turned", tag="bank%d" % TURNED_ELSEWHERE.get(j, j))
             for d in range(PACK):
                 nc.tensor.transpose(turned[:, d, :], relus[j][:, d, :], ident[:])
@@ -195,14 +203,14 @@ def tile_moe_two_mlp_relu2_kernel(
             y = psum.tile([P, C], F32, name="y", tag="bank%d" % (TILES - 1 if e == E - 2 else 2 * e))
             nc.tensor.matmul_mx(
                 out=y[:],
-                lhsT=w2w[:, e, :].bitcast(FP4X4),
+                lhsT=w2w[e].bitcast(FP4X4),
                 lhsT_scale=w2_planes[:, e, :],
                 rhs=h_words[:, slots].bitcast(FP8X4),
                 rhs_scale=h_plane[:, slots],
                 start=True,
                 stop=True,
             )
-            y_sb[e] = keep.tile([P, C], F32, name="y_sb", tag="relu%d" % ((2 * e + 3) % TILES), align_bytes=64)
+            y_sb[e] = keep.tile([P, C], F32, name="y_sb", tag="relu%d" % ((2 * e + 3) % TILES), align_bytes=256)
             nc.scalar.copy(y_sb[e][:], y[:])
 
         def scatter(e):
@@ -230,10 +238,14 @@ def tile_moe_two_mlp_relu2_kernel(
                 turn_and_square(2 * e + 1)
                 quantise(e)
             if ahead and e == 1:
-                finish_sums(2 * e + 2)
+                for o in range(LAST):
+                    first_layer(4, o)
+                    first_layer(5, o)
             if e > 0:
                 second_layer(e - 1)
                 scatter(e - 1)
+            if ahead and e == 1:
+                finish_sums(2 * e + 2)
             if ahead:
                 finish_sums(2 * e + 3)
 

@@ -27,6 +27,7 @@ HALF = SLOTS // 2
 SCALE_ROW = (0, 4, 6)
 PLANE_GROUPS = (range(0, 2 * PASSES + 1), range(2 * PASSES + 1, E * PASSES))
 RELU_ON_VECTOR = (1, 3, 4)
+ALIGN = 256
 TURNED_ELSEWHERE = {0: TILES - 1, TILES - 1: 1}
 
 
@@ -40,20 +41,20 @@ def tile_moe_two_mlp_relu2_kernel(
 
         offs_t = keep.tile([P, SLOTS // 16], U16, name="offs_t")
         dst_t = keep.tile([P, SLOTS // 16], U16, name="dst_t")
-        token_scales = keep.tile([P, T], U8, name="token_scales", tag="window", align_bytes=256)
-        token_words = [keep.tile([P, T], I32, name="token_words%d" % o, align_bytes=256) for o in range(PASSES)]
-        slot_scales = keep.tile([P, SLOTS], U8, name="slot_scales", align_bytes=256)
-        slot_planes = keep.tile([P, LAST, SLOTS], U8, name="slot_planes", align_bytes=256)
-        last_plane = keep.tile([P, SLOTS], U8, name="last_plane", align_bytes=256)
+        token_scales = keep.tile([P, T], U8, name="token_scales", tag="window", align_bytes=ALIGN)
+        token_words = [keep.tile([P, T], I32, name="token_words%d" % o, align_bytes=ALIGN) for o in range(PASSES)]
+        slot_scales = keep.tile([P, SLOTS], U8, name="slot_scales", align_bytes=ALIGN)
+        slot_planes = keep.tile([P, LAST, SLOTS], U8, name="slot_planes", align_bytes=ALIGN)
+        last_plane = keep.tile([P, SLOTS], U8, name="last_plane", align_bytes=ALIGN)
         w1_planes = [
-            keep.tile([P, len(pairs), H], U8, name="w1_planes%d" % n, align_bytes=256)
+            keep.tile([P, len(pairs), H], U8, name="w1_planes%d" % n, align_bytes=ALIGN)
             for n, pairs in enumerate(PLANE_GROUPS)
         ]
-        w2_planes = keep.tile([P, E, N], U8, name="w2_planes", align_bytes=256)
-        gate_t = keep.tile([P, SLOTS], F32, name="gate_t", align_bytes=256)
+        w2_planes = keep.tile([P, E, N], U8, name="w2_planes", align_bytes=ALIGN)
+        gate_t = keep.tile([P, SLOTS], F32, name="gate_t", align_bytes=ALIGN)
         zero = keep.tile([P, 1], F32, name="zero")
-        h_words = keep.tile([P, SLOTS], U32, name="h_words", align_bytes=256)
-        h_plane = keep.tile([P, SLOTS], U8, name="h_plane", align_bytes=256)
+        h_words = keep.tile([P, SLOTS], U32, name="h_words", align_bytes=ALIGN)
+        h_plane = keep.tile([P, SLOTS], U8, name="h_plane", align_bytes=ALIGN)
 
         w1w_hbm = w1_words.rearrange("e s p b -> p (e s) b").bitcast(I32)
         w1s_hbm = w1_scales.rearrange("e s q i -> q (e s) i").bitcast(I32)
@@ -67,7 +68,7 @@ def tile_moe_two_mlp_relu2_kernel(
 
         def load_w1(rows):
             pairs = range(E * PASSES)[rows]
-            words = keep.tile([P, len(pairs), 2 * H], U8, name="w1w%d" % pairs[0], align_bytes=256)
+            words = keep.tile([P, len(pairs), 2 * H], U8, name="w1w%d" % pairs[0], align_bytes=ALIGN)
             nc.sync.dma_start(words[:].bitcast(I32), w1w_hbm[:, rows, :])
             for n, pair in enumerate(pairs):
                 w1w[divmod(pair, PASSES)] = words[:, n, :]
@@ -75,7 +76,7 @@ def tile_moe_two_mlp_relu2_kernel(
         w2w = {}
 
         def load_w2(experts):
-            words = keep.tile([P, len(experts), 2 * N], U8, name="w2w%d" % experts.start, align_bytes=256)
+            words = keep.tile([P, len(experts), 2 * N], U8, name="w2w%d" % experts.start, align_bytes=ALIGN)
             nc.sync.dma_start(words[:].bitcast(I32), w2w_hbm[:, experts.start : experts.stop, :])
             for n, e in enumerate(experts):
                 w2w[e] = words[:, n, :]
@@ -98,7 +99,7 @@ def tile_moe_two_mlp_relu2_kernel(
         slot_words = {}
 
         def gather_words(o, g, width, tag):
-            slot_words[o, g] = keep.tile([P, HALF], U32, name="slot_words", tag=tag, align_bytes=256)
+            slot_words[o, g] = keep.tile([P, HALF], U32, name="slot_words", tag=tag, align_bytes=ALIGN)
             for lo in range(0, HALF, width):
                 chosen = offs_t[:, entries(g * HALF + lo, g * HALF + lo + width)]
                 window = token_words[o][:].bitcast(U32).indirect(chosen)
@@ -107,7 +108,7 @@ def tile_moe_two_mlp_relu2_kernel(
         for sparse in (token_scales, w1_planes[0], slot_planes, w2_planes, last_plane, w1_planes[1]):
             nc.vector.memset(sparse[:].bitcast(I32), 0)
         nc.vector.memset(zero[:], 0.0)
-        ident = keep.tile([P, P], F32, name="ident", align_bytes=256)
+        ident = keep.tile([P, P], F32, name="ident", align_bytes=ALIGN)
         nc.vector.memset(ident[:], 0.0)
         make_identity(nc, ident[:], nomemset=True)
 
@@ -125,15 +126,15 @@ def tile_moe_two_mlp_relu2_kernel(
         nc.vector.tensor_copy(slot_scales[:], token_scales[:].indirect(offs_t[:]))
         move_slot_planes(slot_planes, SCALE_ROW[0], 4)
         load_w1(slice(1, 6, 3))
-        load_planes(w2_planes, w2s_hbm, range(0, 2))
+        load_planes(w2_planes, w2s_hbm, range(0, 1))
         load_tokens(2)
         move_slot_planes(last_plane, SCALE_ROW[LAST], 8)
         load_w1(slice(2, 3))
         load_w1(slice(5, 6))
-        load_w1_planes(1, range(0, 1))
+        load_w1_planes(1, range(0, 2))
         load_w1(slice(6, 9))
-        load_planes(w2_planes, w2s_hbm, range(2, 4))
-        load_w1_planes(1, range(1, 4))
+        load_planes(w2_planes, w2s_hbm, range(1, 4))
+        load_w1_planes(1, range(2, 4))
         load_w2(range(0, 1))
         load_w1(slice(9, 12))
         nc.sync.dma_start(dst_t[:], dst)
@@ -141,7 +142,7 @@ def tile_moe_two_mlp_relu2_kernel(
         load_w2(range(1, E))
         nc.sync.dma_start(gate_t[:, C:SLOTS], gate[:, C:SLOTS])
 
-        placed = keep.tile([P, T], F32, name="placed", tag="window", align_bytes=256)
+        placed = keep.tile([P, T], F32, name="placed", tag="window", align_bytes=ALIGN)
         nc.scalar.activation(placed[:], zero[:].to_broadcast([P, T]), ACT.Square)
 
         sums, relus, h, y_sb = {}, {}, {}, {}
@@ -164,10 +165,14 @@ def tile_moe_two_mlp_relu2_kernel(
                 stop=(o == LAST),
             )
 
+        def early_passes(tiles):
+            for o in range(LAST):
+                for j in tiles:
+                    first_layer(j, o)
+
         def finish_sums(j):
-            for o in range(LAST if j < TILES - 2 else 0, PASSES):
-                first_layer(j, o)
-            relus[j] = keep.tile([P, PACK, P], F32, name="relu", tag="relu%d" % j, align_bytes=256)
+            first_layer(j, LAST)
+            relus[j] = keep.tile([P, PACK, P], F32, name="relu", tag="relu%d" % j, align_bytes=ALIGN)
             by_code = sums[j][:].rearrange("s (p d) -> s d p", d=PACK)
             width = PACK // 2 if j in TURNED_ELSEWHERE else PACK
             for d in range(0, PACK, width):
@@ -180,7 +185,7 @@ def tile_moe_two_mlp_relu2_kernel(
         def turn_and_square(j):
             e = j * P // C
             if j % 2 == 0:
-                h[e] = keep.tile([P, C, PACK], BF16, name="h%d" % e, align_bytes=256)
+                h[e] = keep.tile([P, C, PACK], BF16, name="h%d" % e, align_bytes=ALIGN)
             turned = psum.tile([P, PACK, P], F32, name="turned", tag="bank%d" % TURNED_ELSEWHERE.get(j, j))
             for d in range(PACK):
                 nc.tensor.transpose(turned[:, d, :], relus[j][:, d, :], ident[:])
@@ -210,7 +215,7 @@ def tile_moe_two_mlp_relu2_kernel(
                 start=True,
                 stop=True,
             )
-            y_sb[e] = keep.tile([P, C], F32, name="y_sb", tag="relu%d" % ((2 * e + 3) % TILES), align_bytes=256)
+            y_sb[e] = keep.tile([P, C], F32, name="y_sb", tag="relu%d" % ((2 * e + 3) % TILES), align_bytes=ALIGN)
             nc.scalar.copy(y_sb[e][:], y[:])
 
         def scatter(e):
@@ -227,27 +232,32 @@ def tile_moe_two_mlp_relu2_kernel(
         for j in range(TILES // 2):
             finish_sums(j)
 
-        for e in range(E + 1):
-            ahead = E // 2 <= e + 1 < E
-            if ahead and e > 1:
-                finish_sums(2 * e + 2)
-            if e < E:
-                turn_and_square(2 * e)
-                if e == 0:
-                    gather_words(LAST, 1, C, "relu0")
-                turn_and_square(2 * e + 1)
-                quantise(e)
-            if ahead and e == 1:
-                for o in range(LAST):
-                    first_layer(4, o)
-                    first_layer(5, o)
-            if e > 0:
-                second_layer(e - 1)
-                scatter(e - 1)
-            if ahead and e == 1:
-                finish_sums(2 * e + 2)
-            if ahead:
-                finish_sums(2 * e + 3)
+        def hidden(e):
+            turn_and_square(2 * e)
+            if e == 0:
+                gather_words(LAST, 1, C, "relu0")
+            turn_and_square(2 * e + 1)
+            quantise(e)
+
+        def results(e):
+            second_layer(e)
+            scatter(e)
+
+        hidden(0)
+        hidden(1)
+        early_passes((4, 5))
+        results(0)
+        finish_sums(4)
+        finish_sums(5)
+        early_passes((6,))
+        finish_sums(6)
+        hidden(2)
+        results(1)
+        early_passes((7,))
+        finish_sums(7)
+        hidden(3)
+        results(2)
+        results(3)
 
         nc.sync.dma_start(out[:, 0 : T // 2], placed[:, 0 : T // 2])
         nc.scalar.dma_start(out[:, T // 2 : T], placed[:, T // 2 : T])

@@ -16,6 +16,7 @@ FP8X4 = mybir.dt.float8_e4m3fn_x4
 FP4X4 = mybir.dt.float4_e2m1fn_x4
 ACT = mybir.ActivationFunctionType
 MULT = mybir.AluOpType.mult
+ADD = mybir.AluOpType.add
 
 P = 128
 PACK = 4
@@ -24,11 +25,13 @@ LAST = PASSES - 1
 SLOTS = E * C
 TILES = SLOTS // P
 HALF = SLOTS // 2
-SCALE_ROW = (0, 4, 6)
+LAST_ROWS, EARLY_ROWS, FREE_ROWS = 16, 32, 64
+QUADRANTS = (0, 2, 1, 3)
 PLANE_GROUPS = (range(0, 2 * PASSES + 1), range(2 * PASSES + 1, E * PASSES))
-RELU_ON_VECTOR = (1, 3, 4)
+RELU_ON_VECTOR = (1, 3)
 ALIGN = 256
 TURNED_ELSEWHERE = {0: TILES - 1, TILES - 1: 1}
+PIECES = (256, 512, 512, 512, 256)
 
 
 def tile_moe_two_mlp_relu2_kernel(
@@ -41,7 +44,7 @@ def tile_moe_two_mlp_relu2_kernel(
 
         offs_t = keep.tile([P, SLOTS // 16], U16, name="offs_t")
         dst_t = keep.tile([P, SLOTS // 16], U16, name="dst_t")
-        token_scales = keep.tile([P, T], U8, name="token_scales", tag="window", align_bytes=ALIGN)
+        token_scales = keep.tile([P, T], U8, name="token_scales", align_bytes=ALIGN)
         token_words = [keep.tile([P, T], I32, name="token_words%d" % o, align_bytes=ALIGN) for o in range(PASSES)]
         slot_scales = keep.tile([P, SLOTS], U8, name="slot_scales", align_bytes=ALIGN)
         slot_planes = keep.tile([P, LAST, SLOTS], U8, name="slot_planes", align_bytes=ALIGN)
@@ -52,7 +55,7 @@ def tile_moe_two_mlp_relu2_kernel(
         ]
         w2_planes = keep.tile([P, E, N], U8, name="w2_planes", align_bytes=ALIGN)
         gate_t = keep.tile([P, SLOTS], F32, name="gate_t", align_bytes=ALIGN)
-        zero = keep.tile([P, 1], F32, name="zero")
+        zero = keep.tile([P, P], F32, name="zero", align_bytes=ALIGN)
         h_words = keep.tile([P, SLOTS], U32, name="h_words", align_bytes=ALIGN)
         h_plane = keep.tile([P, SLOTS], U8, name="h_plane", align_bytes=ALIGN)
 
@@ -88,10 +91,10 @@ def tile_moe_two_mlp_relu2_kernel(
         def load_w1_planes(n, rs=range(PACK)):
             load_planes(w1_planes[n], w1s_hbm[:, PLANE_GROUPS[n].start : PLANE_GROUPS[n].stop, :], rs)
 
-        def move_slot_planes(planes, first, step):
-            for r in range(PACK):
-                rows = slot_scales[32 * r + first : 32 * r + 32 : step, :]
-                nc.sync.dma_start(planes[r:P:32].bitcast(I32), rows.bitcast(I32))
+        def move_slot_planes(planes, first, passes):
+            for a in QUADRANTS:
+                rows = slot_scales[first + PACK * passes * a : first + PACK * passes * (a + 1), :]
+                nc.sync.dma_start(planes[32 * a : 32 * a + PACK].bitcast(I32), rows.bitcast(I32))
 
         def entries(lo, hi):
             return slice(lo // 16, hi // 16)
@@ -105,30 +108,33 @@ def tile_moe_two_mlp_relu2_kernel(
                 window = token_words[o][:].bitcast(U32).indirect(chosen)
                 nc.vector.tensor_copy(slot_words[o, g][:, lo : lo + width], window)
 
-        for sparse in (token_scales, w1_planes[0], slot_planes, w2_planes, last_plane, w1_planes[1]):
-            nc.vector.memset(sparse[:].bitcast(I32), 0)
+        nc.vector.memset(w1_planes[0][:].bitcast(I32), 0)
         nc.vector.memset(zero[:], 0.0)
+        nc.vector.memset(token_scales[0:LAST_ROWS, :].bitcast(I32), 0)
+        nc.vector.memset(token_scales[FREE_ROWS:P, :].bitcast(I32), 0)
+        nc.vector.memset(slot_planes[:].bitcast(I32), 0)
         ident = keep.tile([P, P], F32, name="ident", align_bytes=ALIGN)
-        nc.vector.memset(ident[:], 0.0)
-        make_identity(nc, ident[:], nomemset=True)
+        for sparse in (w2_planes, last_plane, w1_planes[1]):
+            nc.gpsimd.memset(sparse[:].bitcast(I32), 0)
+        make_identity(nc, ident[:])
 
+        nc.sync.dma_start(
+            token_scales[EARLY_ROWS:FREE_ROWS, :].bitcast(I32),
+            x_scales[0:LAST].rearrange("o q t -> q o t").bitcast(I32),
+        )
+        nc.sync.dma_start(token_scales[LAST_ROWS:EARLY_ROWS, :].bitcast(I32), x_scales[LAST].bitcast(I32))
         nc.sync.dma_start(offs_t[:], offs)
-        for o in range(PASSES):
-            nc.scalar.dma_start(
-                token_scales[SCALE_ROW[o] : P : 8, :].bitcast(I32),
-                x_scales[o].rearrange("(a r) t -> r a t", r=PACK).bitcast(I32),
-            )
 
         load_tokens(0)
         load_w1_planes(0)
         load_tokens(1)
         load_w1(slice(0, 6, 3))
         nc.vector.tensor_copy(slot_scales[:], token_scales[:].indirect(offs_t[:]))
-        move_slot_planes(slot_planes, SCALE_ROW[0], 4)
+        move_slot_planes(slot_planes, EARLY_ROWS, LAST)
         load_w1(slice(1, 6, 3))
         load_planes(w2_planes, w2s_hbm, range(0, 1))
         load_tokens(2)
-        move_slot_planes(last_plane, SCALE_ROW[LAST], 8)
+        move_slot_planes(last_plane, LAST_ROWS, 1)
         load_w1(slice(2, 3))
         load_w1(slice(5, 6))
         load_w1_planes(1, range(0, 2))
@@ -142,10 +148,12 @@ def tile_moe_two_mlp_relu2_kernel(
         load_w2(range(1, E))
         nc.sync.dma_start(gate_t[:, C:SLOTS], gate[:, C:SLOTS])
 
-        placed = keep.tile([P, T], F32, name="placed", tag="window", align_bytes=ALIGN)
-        nc.scalar.activation(placed[:], zero[:].to_broadcast([P, T]), ACT.Square)
+        placed = keep.tile([P, T], F32, name="placed", align_bytes=ALIGN)
+        placed_by_scalar = keep.tile([P, T], F32, name="placed_by_scalar", align_bytes=ALIGN)
+        for window in (placed, placed_by_scalar):
+            nc.scalar.activation(window[:], zero[:, 0:1].to_broadcast([P, T]), ACT.Square)
 
-        sums, relus, h, y_sb = {}, {}, {}, {}
+        sums, relus, h = {}, {}, {}
 
         def first_layer(j, o):
             if o == 0:
@@ -203,9 +211,9 @@ def tile_moe_two_mlp_relu2_kernel(
                     in_=h[e][:, lo : lo + width, :].rearrange("p s d -> p (s d)"),
                 )
 
-        def second_layer(e):
-            slots = slice(e * C, (e + 1) * C)
-            y = psum.tile([P, C], F32, name="y", tag="bank%d" % (TILES - 1 if e == E - 2 else 2 * e))
+        def second_layer(slots, bank):
+            e = slots.start // C
+            y = psum.tile([P, slots.stop - slots.start], F32, name="y", tag="bank%d" % bank)
             nc.tensor.matmul_mx(
                 out=y[:],
                 lhsT=w2w[e].bitcast(FP4X4),
@@ -215,12 +223,23 @@ def tile_moe_two_mlp_relu2_kernel(
                 start=True,
                 stop=True,
             )
-            y_sb[e] = keep.tile([P, C], F32, name="y_sb", tag="relu%d" % ((2 * e + 3) % TILES), align_bytes=ALIGN)
-            nc.scalar.copy(y_sb[e][:], y[:])
+            return y
 
-        def scatter(e):
-            window = placed[:].indirect(dst_t[:, entries(e * C, (e + 1) * C)])
-            nc.vector.tensor_tensor(window, y_sb[e][:], gate_t[:, e * C : (e + 1) * C], MULT)
+        def places(window, slots):
+            return window[:].indirect(dst_t[:, entries(slots.start, slots.stop)])
+
+        def early_results(e):
+            slots = slice(e * C, (e + 1) * C)
+            y = second_layer(slots, 2 * e)
+            y_sb = keep.tile([P, C], F32, name="y_sb", tag="relu%d" % (2 * e + 3), align_bytes=ALIGN)
+            nc.scalar.copy(y_sb[:], y[:])
+            nc.vector.tensor_tensor(places(placed, slots), y_sb[:], gate_t[:, slots], MULT)
+
+        def gated_results(slots, bank, tag):
+            y = second_layer(slots, bank)
+            gated = keep.tile([P, slots.stop - slots.start], F32, name="gated", tag=tag, align_bytes=ALIGN)
+            nc.vector.tensor_tensor(gated[:], y[:], gate_t[:, slots], MULT)
+            return gated
 
         for o in range(LAST):
             for g in range(2):
@@ -239,25 +258,32 @@ def tile_moe_two_mlp_relu2_kernel(
             turn_and_square(2 * e + 1)
             quantise(e)
 
-        def results(e):
-            second_layer(e)
-            scatter(e)
-
         hidden(0)
         hidden(1)
         early_passes((4, 5))
-        results(0)
+        early_results(0)
         finish_sums(4)
         finish_sums(5)
         early_passes((6,))
         finish_sums(6)
         hidden(2)
-        results(1)
+        early_results(1)
         early_passes((7,))
         finish_sums(7)
         hidden(3)
-        results(2)
-        results(3)
 
-        nc.sync.dma_start(out[:, 0 : T // 2], placed[:, 0 : T // 2])
-        nc.scalar.dma_start(out[:, T // 2 : T], placed[:, T // 2 : T])
+        slots = slice(2 * C, 3 * C)
+        gated = gated_results(slots, TILES - 1, "relu%d" % (TILES - 1))
+        nc.scalar.activation(places(placed_by_scalar, slots), gated[:], ACT.Copy)
+        for j in (TILES - 2, TILES - 1):
+            slots = slice(j * P, (j + 1) * P)
+            gated = gated_results(slots, j - 2, "gated%d" % j)
+            nc.vector.tensor_tensor(places(placed, slots), gated[:], zero[:], ADD)
+
+        lo = 0
+        for n, width in enumerate(PIECES):
+            total = keep.tile([P, width], F32, name="total%d" % n, align_bytes=ALIGN)
+            nc.vector.tensor_tensor(total[:], placed[:, lo : lo + width], placed_by_scalar[:, lo : lo + width], ADD)
+            queue = nc.scalar if n % 2 else nc.sync
+            queue.dma_start(out[:, lo : lo + width], total[:])
+            lo = lo + width

@@ -16,7 +16,6 @@ FP8X4 = mybir.dt.float8_e4m3fn_x4
 FP4X4 = mybir.dt.float4_e2m1fn_x4
 ACT = mybir.ActivationFunctionType
 MULT = mybir.AluOpType.mult
-ADD = mybir.AluOpType.add
 
 P = 128
 PACK = 4
@@ -28,10 +27,9 @@ HALF = SLOTS // 2
 LAST_ROWS, EARLY_ROWS, FREE_ROWS = 16, 32, 64
 QUADRANTS = (0, 2, 1, 3)
 PLANE_GROUPS = (range(0, 2 * PASSES + 1), range(2 * PASSES + 1, E * PASSES))
-RELU_ON_VECTOR = (1, 3)
+RELU_ON_VECTOR = (1, 3, 4)
 ALIGN = 256
 TURNED_ELSEWHERE = {0: TILES - 1, TILES - 1: 1}
-PIECES = (256, 512, 512, 512, 256)
 
 
 def tile_moe_two_mlp_relu2_kernel(
@@ -55,7 +53,7 @@ def tile_moe_two_mlp_relu2_kernel(
         ]
         w2_planes = keep.tile([P, E, N], U8, name="w2_planes", align_bytes=ALIGN)
         gate_t = keep.tile([P, SLOTS], F32, name="gate_t", align_bytes=ALIGN)
-        zero = keep.tile([P, P], F32, name="zero", align_bytes=ALIGN)
+        zero = keep.tile([P, 1], F32, name="zero")
         h_words = keep.tile([P, SLOTS], U32, name="h_words", align_bytes=ALIGN)
         h_plane = keep.tile([P, SLOTS], U8, name="h_plane", align_bytes=ALIGN)
 
@@ -149,11 +147,9 @@ def tile_moe_two_mlp_relu2_kernel(
         nc.sync.dma_start(gate_t[:, C:SLOTS], gate[:, C:SLOTS])
 
         placed = keep.tile([P, T], F32, name="placed", align_bytes=ALIGN)
-        placed_by_scalar = keep.tile([P, T], F32, name="placed_by_scalar", align_bytes=ALIGN)
-        for window in (placed, placed_by_scalar):
-            nc.scalar.activation(window[:], zero[:, 0:1].to_broadcast([P, T]), ACT.Square)
+        nc.scalar.activation(placed[:], zero[:].to_broadcast([P, T]), ACT.Square)
 
-        sums, relus, h = {}, {}, {}
+        sums, relus, h, y_sb = {}, {}, {}, {}
 
         def first_layer(j, o):
             if o == 0:
@@ -211,9 +207,9 @@ def tile_moe_two_mlp_relu2_kernel(
                     in_=h[e][:, lo : lo + width, :].rearrange("p s d -> p (s d)"),
                 )
 
-        def second_layer(slots, bank):
-            e = slots.start // C
-            y = psum.tile([P, slots.stop - slots.start], F32, name="y", tag="bank%d" % bank)
+        def second_layer(e):
+            slots = slice(e * C, (e + 1) * C)
+            y = psum.tile([P, C], F32, name="y", tag="bank%d" % (TILES - 1 if e == E - 2 else 2 * e))
             nc.tensor.matmul_mx(
                 out=y[:],
                 lhsT=w2w[e].bitcast(FP4X4),
@@ -223,23 +219,12 @@ def tile_moe_two_mlp_relu2_kernel(
                 start=True,
                 stop=True,
             )
-            return y
+            y_sb[e] = keep.tile([P, C], F32, name="y_sb", tag="relu%d" % ((2 * e + 3) % TILES), align_bytes=ALIGN)
+            nc.scalar.copy(y_sb[e][:], y[:])
 
-        def places(window, slots):
-            return window[:].indirect(dst_t[:, entries(slots.start, slots.stop)])
-
-        def early_results(e):
-            slots = slice(e * C, (e + 1) * C)
-            y = second_layer(slots, 2 * e)
-            y_sb = keep.tile([P, C], F32, name="y_sb", tag="relu%d" % (2 * e + 3), align_bytes=ALIGN)
-            nc.scalar.copy(y_sb[:], y[:])
-            nc.vector.tensor_tensor(places(placed, slots), y_sb[:], gate_t[:, slots], MULT)
-
-        def gated_results(slots, bank, tag):
-            y = second_layer(slots, bank)
-            gated = keep.tile([P, slots.stop - slots.start], F32, name="gated", tag=tag, align_bytes=ALIGN)
-            nc.vector.tensor_tensor(gated[:], y[:], gate_t[:, slots], MULT)
-            return gated
+        def scatter(e):
+            window = placed[:].indirect(dst_t[:, entries(e * C, (e + 1) * C)])
+            nc.vector.tensor_tensor(window, y_sb[e][:], gate_t[:, e * C : (e + 1) * C], MULT)
 
         for o in range(LAST):
             for g in range(2):
@@ -258,32 +243,25 @@ def tile_moe_two_mlp_relu2_kernel(
             turn_and_square(2 * e + 1)
             quantise(e)
 
+        def results(e):
+            second_layer(e)
+            scatter(e)
+
         hidden(0)
         hidden(1)
         early_passes((4, 5))
-        early_results(0)
+        results(0)
         finish_sums(4)
         finish_sums(5)
         early_passes((6,))
         finish_sums(6)
         hidden(2)
-        early_results(1)
+        results(1)
         early_passes((7,))
         finish_sums(7)
         hidden(3)
+        results(2)
+        results(3)
 
-        slots = slice(2 * C, 3 * C)
-        gated = gated_results(slots, TILES - 1, "relu%d" % (TILES - 1))
-        nc.scalar.activation(places(placed_by_scalar, slots), gated[:], ACT.Copy)
-        for j in (TILES - 2, TILES - 1):
-            slots = slice(j * P, (j + 1) * P)
-            gated = gated_results(slots, j - 2, "gated%d" % j)
-            nc.vector.tensor_tensor(places(placed, slots), gated[:], zero[:], ADD)
-
-        lo = 0
-        for n, width in enumerate(PIECES):
-            total = keep.tile([P, width], F32, name="total%d" % n, align_bytes=ALIGN)
-            nc.vector.tensor_tensor(total[:], placed[:, lo : lo + width], placed_by_scalar[:, lo : lo + width], ADD)
-            queue = nc.scalar if n % 2 else nc.sync
-            queue.dma_start(out[:, lo : lo + width], total[:])
-            lo = lo + width
+        nc.sync.dma_start(out[:, 0 : T // 2], placed[:, 0 : T // 2])
+        nc.scalar.dma_start(out[:, T // 2 : T], placed[:, T // 2 : T])

@@ -45,7 +45,7 @@ def tile_moe_two_mlp_relu2_kernel(
         token_scales = keep.tile([P, T], U8, name="token_scales", align_bytes=ALIGN)
         token_words = [keep.tile([P, T], I32, name="token_words%d" % o, align_bytes=ALIGN) for o in range(PASSES)]
         slot_scales = keep.tile([P, SLOTS], U8, name="slot_scales", align_bytes=ALIGN)
-        slot_planes = keep.tile([P, LAST, SLOTS], U8, name="slot_planes", align_bytes=ALIGN)
+        slot_planes = [keep.tile([P, LAST, HALF], U8, name="slot_planes%d" % g, align_bytes=ALIGN) for g in range(2)]
         last_plane = keep.tile([P, SLOTS], U8, name="last_plane", align_bytes=ALIGN)
         w1_planes = [
             keep.tile([P, len(pairs), H], U8, name="w1_planes%d" % n, align_bytes=ALIGN)
@@ -82,9 +82,9 @@ def tile_moe_two_mlp_relu2_kernel(
             for n, e in enumerate(experts):
                 w2w[e] = words[:, n, :]
 
-        def load_planes(planes, rows, rs=range(PACK)):
+        def load_planes(planes, rows, rs=range(PACK), queue=nc.sync):
             for r in rs:
-                nc.sync.dma_start(planes[r:P:32].bitcast(I32), rows[r:16:PACK])
+                queue.dma_start(planes[r:P:32].bitcast(I32), rows[r:16:PACK])
 
         def load_w1_planes(n, rs=range(PACK)):
             load_planes(w1_planes[n], w1s_hbm[:, PLANE_GROUPS[n].start : PLANE_GROUPS[n].stop, :], rs)
@@ -93,6 +93,11 @@ def tile_moe_two_mlp_relu2_kernel(
             for a in QUADRANTS:
                 rows = slot_scales[first + PACK * passes * a : first + PACK * passes * (a + 1), :]
                 nc.sync.dma_start(planes[32 * a : 32 * a + PACK].bitcast(I32), rows.bitcast(I32))
+
+        def move_half_planes(g):
+            for a in QUADRANTS:
+                rows = slot_scales[EARLY_ROWS + 8 * a : EARLY_ROWS + 8 * (a + 1), g * HALF : (g + 1) * HALF]
+                nc.sync.dma_start(slot_planes[g][32 * a : 32 * a + PACK].bitcast(I32), rows.bitcast(I32))
 
         def entries(lo, hi):
             return slice(lo // 16, hi // 16)
@@ -110,11 +115,12 @@ def tile_moe_two_mlp_relu2_kernel(
         nc.vector.memset(zero[:], 0.0)
         nc.vector.memset(token_scales[0:LAST_ROWS, :].bitcast(I32), 0)
         nc.vector.memset(token_scales[FREE_ROWS:P, :].bitcast(I32), 0)
-        nc.vector.memset(slot_planes[:].bitcast(I32), 0)
+        nc.vector.memset(slot_planes[0][:].bitcast(I32), 0)
         ident = keep.tile([P, P], F32, name="ident", align_bytes=ALIGN)
-        for sparse in (w2_planes, last_plane, w1_planes[1]):
+        for sparse in (w2_planes, last_plane, slot_planes[1], w1_planes[1]):
             nc.gpsimd.memset(sparse[:].bitcast(I32), 0)
         make_identity(nc, ident[:])
+        load_planes(w2_planes, w2s_hbm, queue=nc.gpsimd)
 
         nc.sync.dma_start(
             token_scales[EARLY_ROWS:FREE_ROWS, :].bitcast(I32),
@@ -128,20 +134,19 @@ def tile_moe_two_mlp_relu2_kernel(
         load_tokens(1)
         load_w1(slice(0, 6, 3))
         nc.vector.tensor_copy(slot_scales[:], token_scales[:].indirect(offs_t[:]))
-        move_slot_planes(slot_planes, EARLY_ROWS, LAST)
+        move_half_planes(0)
         load_w1(slice(1, 6, 3))
-        load_planes(w2_planes, w2s_hbm, range(0, 1))
+        nc.sync.dma_start(dst_t[:], dst)
         load_tokens(2)
         move_slot_planes(last_plane, LAST_ROWS, 1)
         load_w1(slice(2, 3))
         load_w1(slice(5, 6))
+        move_half_planes(1)
         load_w1_planes(1, range(0, 2))
         load_w1(slice(6, 9))
-        load_planes(w2_planes, w2s_hbm, range(1, 4))
         load_w1_planes(1, range(2, 4))
         load_w2(range(0, 1))
         load_w1(slice(9, 12))
-        nc.sync.dma_start(dst_t[:], dst)
         nc.sync.dma_start(gate_t[:, 0:C], gate[:, 0:C])
         load_w2(range(1, E))
         nc.sync.dma_start(gate_t[:, C:SLOTS], gate[:, C:SLOTS])
@@ -162,7 +167,7 @@ def tile_moe_two_mlp_relu2_kernel(
             nc.tensor.matmul_mx(
                 out=sums[j][:],
                 lhsT=slot_words[o, g][:, in_half].bitcast(FP8X4),
-                lhsT_scale=last_plane[:, slots] if o == LAST else slot_planes[:, o, slots],
+                lhsT_scale=last_plane[:, slots] if o == LAST else slot_planes[g][:, o, in_half],
                 rhs=w1w[e, o].bitcast(FP4X4),
                 rhs_scale=w1_planes[n][:, pair - PLANE_GROUPS[n].start, :],
                 start=(o == 0),

@@ -136,7 +136,6 @@ def tile_moe_two_mlp_relu2_kernel(
         nc.vector.tensor_copy(slot_scales[:], token_scales[:].indirect(offs_t[:]))
         move_half_planes(0)
         load_w1(slice(1, 6, 3))
-        nc.sync.dma_start(dst_t[:], dst)
         load_tokens(2)
         move_slot_planes(last_plane, LAST_ROWS, 1)
         load_w1(slice(2, 3))
@@ -147,6 +146,7 @@ def tile_moe_two_mlp_relu2_kernel(
         load_w1_planes(1, range(2, 4))
         load_w2(range(0, 1))
         load_w1(slice(9, 12))
+        nc.sync.dma_start(dst_t[:], dst)
         nc.sync.dma_start(gate_t[:, 0:C], gate[:, 0:C])
         load_w2(range(1, E))
         nc.sync.dma_start(gate_t[:, C:SLOTS], gate[:, C:SLOTS])

@@ -27,9 +27,11 @@ HALF = SLOTS // 2
 LAST_ROWS, EARLY_ROWS, FREE_ROWS = 16, 32, 64
 QUADRANTS = (0, 2, 1, 3)
 PLANE_GROUPS = (range(0, 2 * PASSES + 1), range(2 * PASSES + 1, E * PASSES))
+MOVE_GROUPS = (slice(0, 3 * C), slice(3 * C, SLOTS))
 RELU_ON_VECTOR = (1, 3, 4)
 ALIGN = 256
 TURNED_ELSEWHERE = {0: TILES - 1, TILES - 1: 1}
+CODES_TAG = {1: "relu0"}
 
 
 def tile_moe_two_mlp_relu2_kernel(
@@ -45,7 +47,10 @@ def tile_moe_two_mlp_relu2_kernel(
         token_scales = keep.tile([P, T], U8, name="token_scales", align_bytes=ALIGN)
         token_words = [keep.tile([P, T], I32, name="token_words%d" % o, align_bytes=ALIGN) for o in range(PASSES)]
         slot_scales = keep.tile([P, SLOTS], U8, name="slot_scales", align_bytes=ALIGN)
-        slot_planes = [keep.tile([P, LAST, HALF], U8, name="slot_planes%d" % g, align_bytes=ALIGN) for g in range(2)]
+        slot_planes = [
+            keep.tile([P, LAST, cols.stop - cols.start], U8, name="slot_planes%d" % n, align_bytes=ALIGN)
+            for n, cols in enumerate(MOVE_GROUPS)
+        ]
         last_plane = keep.tile([P, SLOTS], U8, name="last_plane", align_bytes=ALIGN)
         w1_planes = [
             keep.tile([P, len(pairs), H], U8, name="w1_planes%d" % n, align_bytes=ALIGN)
@@ -54,7 +59,7 @@ def tile_moe_two_mlp_relu2_kernel(
         w2_planes = keep.tile([P, E, N], U8, name="w2_planes", align_bytes=ALIGN)
         gate_t = keep.tile([P, SLOTS], F32, name="gate_t", align_bytes=ALIGN)
         zero = keep.tile([P, 1], F32, name="zero")
-        h_words = keep.tile([P, SLOTS], U32, name="h_words", align_bytes=ALIGN)
+        h_words = {}
         h_plane = keep.tile([P, SLOTS], U8, name="h_plane", align_bytes=ALIGN)
 
         w1w_hbm = w1_words.rearrange("e s p b -> p (e s) b").bitcast(I32)
@@ -96,13 +101,21 @@ def tile_moe_two_mlp_relu2_kernel(
 
         def move_half_planes(g):
             for a in QUADRANTS:
-                rows = slot_scales[EARLY_ROWS + 8 * a : EARLY_ROWS + 8 * (a + 1), g * HALF : (g + 1) * HALF]
+                rows = slot_scales[EARLY_ROWS + 8 * a : EARLY_ROWS + 8 * (a + 1), MOVE_GROUPS[g]]
                 nc.sync.dma_start(slot_planes[g][32 * a : 32 * a + PACK].bitcast(I32), rows.bitcast(I32))
 
         def entries(lo, hi):
             return slice(lo // 16, hi // 16)
 
         slot_words = {}
+        last_words = {}
+
+        def gather_last(tiles, tag):
+            words = keep.tile([P, len(tiles) * P], U32, name="last_words", tag=tag, align_bytes=ALIGN)
+            chosen = offs_t[:, entries(tiles.start * P, tiles.stop * P)]
+            nc.vector.tensor_copy(words[:], token_words[LAST][:].bitcast(U32).indirect(chosen))
+            for n, j in enumerate(tiles):
+                last_words[j] = words[:, n * P : (n + 1) * P]
 
         def gather_words(o, g, width, tag):
             slot_words[o, g] = keep.tile([P, HALF], U32, name="slot_words", tag=tag, align_bytes=ALIGN)
@@ -139,13 +152,12 @@ def tile_moe_two_mlp_relu2_kernel(
         load_tokens(2)
         move_slot_planes(last_plane, LAST_ROWS, 1)
         load_w1(slice(2, 3))
-        load_w1(slice(5, 6))
+        load_w1(slice(5, 7))
         move_half_planes(1)
-        load_w1_planes(1, range(0, 2))
-        load_w1(slice(6, 9))
-        load_w1_planes(1, range(2, 4))
-        load_w2(range(0, 1))
+        load_w1_planes(1)
+        load_w1(slice(7, 9))
         load_w1(slice(9, 12))
+        load_w2(range(0, 1))
         nc.sync.dma_start(dst_t[:], dst)
         nc.sync.dma_start(gate_t[:, 0:C], gate[:, 0:C])
         load_w2(range(1, E))
@@ -162,12 +174,14 @@ def tile_moe_two_mlp_relu2_kernel(
             e, g = j * P // C, j * P // HALF
             in_half = slice(j * P - g * HALF, (j + 1) * P - g * HALF)
             slots = slice(j * P, (j + 1) * P)
+            m = int(e == E - 1)
+            in_group = slice(slots.start - MOVE_GROUPS[m].start, slots.stop - MOVE_GROUPS[m].start)
             pair = PASSES * e + o
             n = int(pair in PLANE_GROUPS[1])
             nc.tensor.matmul_mx(
                 out=sums[j][:],
-                lhsT=slot_words[o, g][:, in_half].bitcast(FP8X4),
-                lhsT_scale=last_plane[:, slots] if o == LAST else slot_planes[g][:, o, in_half],
+                lhsT=(last_words[j] if o == LAST else slot_words[o, g][:, in_half]).bitcast(FP8X4),
+                lhsT_scale=last_plane[:, slots] if o == LAST else slot_planes[m][:, o, in_group],
                 rhs=w1w[e, o].bitcast(FP4X4),
                 rhs_scale=w1_planes[n][:, pair - PLANE_GROUPS[n].start, :],
                 start=(o == 0),
@@ -204,10 +218,11 @@ def tile_moe_two_mlp_relu2_kernel(
 
         def quantise(e):
             width = P if e == E - 1 else C
+            h_words[e] = keep.tile([P, C], U32, name="h_words", tag=CODES_TAG.get(e, "h_words%d" % e), align_bytes=ALIGN)
             for lo in range(0, C, width):
                 slots = slice(e * C + lo, e * C + lo + width)
                 nc.vector.quantize_mx(
-                    out=h_words[:, slots].bitcast(FP8X4),
+                    out=h_words[e][:, lo : lo + width].bitcast(FP8X4),
                     scales=h_plane[:, slots],
                     in_=h[e][:, lo : lo + width, :].rearrange("p s d -> p (s d)"),
                 )
@@ -219,7 +234,7 @@ def tile_moe_two_mlp_relu2_kernel(
                 out=y[:],
                 lhsT=w2w[e].bitcast(FP4X4),
                 lhsT_scale=w2_planes[:, e, :],
-                rhs=h_words[:, slots].bitcast(FP8X4),
+                rhs=h_words[e][:].bitcast(FP8X4),
                 rhs_scale=h_plane[:, slots],
                 start=True,
                 stop=True,
@@ -237,14 +252,15 @@ def tile_moe_two_mlp_relu2_kernel(
             for j in range(TILES // 2):
                 first_layer(j, o)
 
-        gather_words(LAST, 0, P, "slot_words%d0" % LAST)
+        for j in range(TILES // 2):
+            gather_last(range(j, j + 1), "last_words%d" % j)
         for j in range(TILES // 2):
             finish_sums(j)
 
+        first_layer(4, 0)
+
         def hidden(e):
             turn_and_square(2 * e)
-            if e == 0:
-                gather_words(LAST, 1, C, "relu0")
             turn_and_square(2 * e + 1)
             quantise(e)
 
@@ -252,12 +268,21 @@ def tile_moe_two_mlp_relu2_kernel(
             second_layer(e)
             scatter(e)
 
-        hidden(0)
-        hidden(1)
-        early_passes((4, 5))
-        results(0)
+        turn_and_square(0)
+        gather_last(range(4, 5), "relu0")
+        turn_and_square(1)
+        gather_last(range(5, 6), "relu1")
+        quantise(0)
+        turn_and_square(2)
+        gather_last(range(6, 8), "relu2")
+        turn_and_square(3)
+        first_layer(5, 0)
+        first_layer(4, 1)
         finish_sums(4)
+        quantise(1)
+        first_layer(5, 1)
         finish_sums(5)
+        results(0)
         early_passes((6,))
         finish_sums(6)
         hidden(2)

@@ -67,8 +67,8 @@ def tile_moe_two_mlp_relu2_kernel(
         w2w_hbm = w2_words.rearrange("e s p b -> p (e s) b").bitcast(I32)
         w2s_hbm = w2_scales.rearrange("e s q n -> q (e s) n").bitcast(I32)
 
-        def load_tokens(o):
-            nc.sync.dma_start(token_words[o][:], x_words[o].rearrange("p t r -> p (t r)").bitcast(I32))
+        def load_tokens(o, cols=slice(0, T)):
+            nc.sync.dma_start(token_words[o][:, cols], x_words[o].rearrange("p t r -> p (t r)").bitcast(I32)[:, cols])
 
         w1w = {}
 
@@ -144,10 +144,11 @@ def tile_moe_two_mlp_relu2_kernel(
 
         load_tokens(0)
         load_w1_planes(0)
-        load_tokens(1)
         load_w1(slice(0, 6, 3))
+        load_tokens(1, slice(0, T // 2))
         nc.vector.tensor_copy(slot_scales[:], token_scales[:].indirect(offs_t[:]))
         move_half_planes(0)
+        load_tokens(1, slice(T // 2, T))
         load_w1(slice(1, 6, 3))
         load_tokens(2)
         move_slot_planes(last_plane, LAST_ROWS, 1)

from contextlib import ExitStack

import concourse.mybir as mybir
from concourse.masks import make_identity

K, T, E, C, H, N = 1536, 2048, 4, 256, 512, 128
FLOPS = 2 * E * C * (K * H + H * N)

F32 = mybir.dt.float32
BF16 = mybir.dt.bfloat16
I32 = mybir.dt.int32
U32 = mybir.dt.uint32
U16 = mybir.dt.uint16
U8 = mybir.dt.uint8
FP8X4 = mybir.dt.float8_e4m3fn_x4
FP4X4 = mybir.dt.float4_e2m1fn_x4
ACT = mybir.ActivationFunctionType
MULT = mybir.AluOpType.mult

P = 128
PACK = 4
PASSES = K // (P * PACK)
LAST = PASSES - 1
SLOTS = E * C
TILES = SLOTS // P
HALF = SLOTS // 2
LAST_ROWS, EARLY_ROWS, FREE_ROWS = 16, 32, 64
QUADRANTS = (0, 2, 1, 3)
PLANE_GROUPS = (range(0, 2 * PASSES + 1), range(2 * PASSES + 1, E * PASSES))
MOVE_GROUPS = (slice(0, 3 * C), slice(3 * C, SLOTS))
RELU_ON_VECTOR = (1, 3, 4)
ALIGN = 256
TURNED_ELSEWHERE = {0: TILES - 1, TILES - 1: 1}
CODES_TAG = {1: "relu0"}


def tile_moe_two_mlp_relu2_kernel(
    tc, x_words, x_scales, w1_words, w1_scales, w2_words, w2_scales, gate, offs, dst, out
):
    nc = tc.nc
    with ExitStack() as ctx:
        keep = ctx.enter_context(tc.tile_pool(name="keep", bufs=1))
        psum = ctx.enter_context(tc.psum_pool(name="psum", bufs=1))

        offs_t = keep.tile([P, SLOTS // 16], U16, name="offs_t")
        dst_t = keep.tile([P, SLOTS // 16], U16, name="dst_t")
        token_scales = keep.tile([P, T], U8, name="token_scales", align_bytes=ALIGN)
        token_words = [keep.tile([P, T], I32, name="token_words%d" % o, align_bytes=ALIGN) for o in range(PASSES)]
        slot_scales = keep.tile([P, SLOTS], U8, name="slot_scales", align_bytes=ALIGN)
        slot_planes = [
            keep.tile([P, LAST, cols.stop - cols.start], U8, name="slot_planes%d" % n, align_bytes=ALIGN)
            for n, cols in enumerate(MOVE_GROUPS)
        ]
        last_plane = keep.tile([P, SLOTS], U8, name="last_plane", align_bytes=ALIGN)
        w1_planes = [
            keep.tile([P, len(pairs), H], U8, name="w1_planes%d" % n, align_bytes=ALIGN)
            for n, pairs in enumerate(PLANE_GROUPS)
        ]
        w2_planes = keep.tile([P, E, N], U8, name="w2_planes", align_bytes=ALIGN)
        gate_t = keep.tile([P, SLOTS], F32, name="gate_t", align_bytes=ALIGN)
        zero = keep.tile([P, 1], F32, name="zero")
        h_words = {}
        h_plane = keep.tile([P, SLOTS], U8, name="h_plane", align_bytes=ALIGN)

        w1w_hbm = w1_words.rearrange("e s p b -> p (e s) b").bitcast(I32)
        w1s_hbm = w1_scales.rearrange("e s q i -> q (e s) i").bitcast(I32)
        w2w_hbm = w2_words.rearrange("e s p b -> p (e s) b").bitcast(I32)
        w2s_hbm = w2_scales.rearrange("e s q n -> q (e s) n").bitcast(I32)

        def load_tokens(o, cols=slice(0, T)):
            nc.sync.dma_start(token_words[o][:, cols], x_words[o].rearrange("p t r -> p (t r)").bitcast(I32)[:, cols])

        w1w = {}

        def load_w1(rows):
            pairs = range(E * PASSES)[rows]
            words = keep.tile([P, len(pairs), 2 * H], U8, name="w1w%d" % pairs[0], align_bytes=ALIGN)
            nc.sync.dma_start(words[:].bitcast(I32), w1w_hbm[:, rows, :])
            for n, pair in enumerate(pairs):
                w1w[divmod(pair, PASSES)] = words[:, n, :]

        w2w = {}

        def load_w2(experts):
            words = keep.tile([P, len(experts), 2 * N], U8, name="w2w%d" % experts.start, align_bytes=ALIGN)
            nc.sync.dma_start(words[:].bitcast(I32), w2w_hbm[:, experts.start : experts.stop, :])
            for n, e in enumerate(experts):
                w2w[e] = words[:, n, :]

        def load_planes(planes, rows, rs=range(PACK), queue=nc.sync):
            for r in rs:
                queue.dma_start(planes[r:P:32].bitcast(I32), rows[r:16:PACK])

        def load_w1_planes(n, rs=range(PACK)):
            load_planes(w1_planes[n], w1s_hbm[:, PLANE_GROUPS[n].start : PLANE_GROUPS[n].stop, :], rs)

        def move_slot_planes(planes, first, passes):
            for a in QUADRANTS:
                rows = slot_scales[first + PACK * passes * a : first + PACK * passes * (a + 1), :]
                nc.sync.dma_start(planes[32 * a : 32 * a + PACK].bitcast(I32), rows.bitcast(I32))

        def move_half_planes(g):
            for a in QUADRANTS:
                rows = slot_scales[EARLY_ROWS + 8 * a : EARLY_ROWS + 8 * (a + 1), MOVE_GROUPS[g]]
                nc.sync.dma_start(slot_planes[g][32 * a : 32 * a + PACK].bitcast(I32), rows.bitcast(I32))

        def entries(lo, hi):
            return slice(lo // 16, hi // 16)

        slot_words = {}
        last_words = {}

        def gather_last(tiles, tag):
            words = keep.tile([P, len(tiles) * P], U32, name="last_words", tag=tag, align_bytes=ALIGN)
            chosen = offs_t[:, entries(tiles.start * P, tiles.stop * P)]
            nc.vector.tensor_copy(words[:], token_words[LAST][:].bitcast(U32).indirect(chosen))
            for n, j in enumerate(tiles):
                last_words[j] = words[:, n * P : (n + 1) * P]

        def gather_words(o, g, width, tag):
            slot_words[o, g] = keep.tile([P, HALF], U32, name="slot_words", tag=tag, align_bytes=ALIGN)
            for lo in range(0, HALF, width):
                chosen = offs_t[:, entries(g * HALF + lo, g * HALF + lo + width)]
                window = token_words[o][:].bitcast(U32).indirect(chosen)
                nc.vector.tensor_copy(slot_words[o, g][:, lo : lo + width], window)

        nc.vector.memset(w1_planes[0][:].bitcast(I32), 0)
        nc.vector.memset(zero[:], 0.0)
        nc.vector.memset(token_scales[0:LAST_ROWS, :].bitcast(I32), 0)
        nc.vector.memset(token_scales[FREE_ROWS:P, :].bitcast(I32), 0)
        nc.vector.memset(slot_planes[0][:].bitcast(I32), 0)
        ident = keep.tile([P, P], F32, name="ident", align_bytes=ALIGN)
        for sparse in (w2_planes, last_plane, slot_planes[1], w1_planes[1]):
            nc.gpsimd.memset(sparse[:].bitcast(I32), 0)
        make_identity(nc, ident[:])
        load_planes(w2_planes, w2s_hbm, queue=nc.gpsimd)

        nc.sync.dma_start(
            token_scales[EARLY_ROWS:FREE_ROWS, :].bitcast(I32),
            x_scales[0:LAST].rearrange("o q t -> q o t").bitcast(I32),
        )
        nc.sync.dma_start(token_scales[LAST_ROWS:EARLY_ROWS, :].bitcast(I32), x_scales[LAST].bitcast(I32))
        nc.sync.dma_start(offs_t[:], offs)

        load_tokens(0)
        load_w1_planes(0)
        load_w1(slice(0, 6, 3))
        load_tokens(1, slice(0, T // 2))
        nc.vector.tensor_copy(slot_scales[:], token_scales[:].indirect(offs_t[:]))
        move_half_planes(0)
        load_tokens(1, slice(T // 2, T))
        load_w1(slice(1, 6, 3))
        load_tokens(2)
        move_slot_planes(last_plane, LAST_ROWS, 1)
        load_w1(slice(2, 3))
        load_w1(slice(5, 7))
        move_half_planes(1)
        load_w1_planes(1)
        load_w1(slice(7, 9))
        load_w1(slice(9, 12))
        load_w2(range(0, 1))
        nc.sync.dma_start(dst_t[:], dst)
        nc.sync.dma_start(gate_t[:, 0:C], gate[:, 0:C])
        load_w2(range(1, E))
        nc.sync.dma_start(gate_t[:, C:SLOTS], gate[:, C:SLOTS])

        placed = keep.tile([P, T], F32, name="placed", align_bytes=ALIGN)
        nc.scalar.activation(placed[:], zero[:].to_broadcast([P, T]), ACT.Square)

        sums, relus, h, y_sb = {}, {}, {}, {}

        def first_layer(j, o):
            if o == 0:
                sums[j] = psum.tile([P, H], F32, name="sums", tag="bank%d" % j)
            e, g = j * P // C, j * P // HALF
            in_half = slice(j * P - g * HALF, (j + 1) * P - g * HALF)
            slots = slice(j * P, (j + 1) * P)
            m = int(e == E - 1)
            in_group = slice(slots.start - MOVE_GROUPS[m].start, slots.stop - MOVE_GROUPS[m].start)
            pair = PASSES * e + o
            n = int(pair in PLANE_GROUPS[1])
            nc.tensor.matmul_mx(
                out=sums[j][:],
                lhsT=(last_words[j] if o == LAST else slot_words[o, g][:, in_half]).bitcast(FP8X4),
                lhsT_scale=last_plane[:, slots] if o == LAST else slot_planes[m][:, o, in_group],
                rhs=w1w[e, o].bitcast(FP4X4),
                rhs_scale=w1_planes[n][:, pair - PLANE_GROUPS[n].start, :],
                start=(o == 0),
                stop=(o == LAST),
            )

        def early_passes(tiles):
            for o in range(LAST):
                for j in tiles:
                    first_layer(j, o)

        def finish_sums(j):
            first_layer(j, LAST)
            relus[j] = keep.tile([P, PACK, P], F32, name="relu", tag="relu%d" % j, align_bytes=ALIGN)
            by_code = sums[j][:].rearrange("s (p d) -> s d p", d=PACK)
            width = PACK // 2 if j in TURNED_ELSEWHERE else PACK
            for d in range(0, PACK, width):
                codes = slice(d, d + width)
                if j in RELU_ON_VECTOR:
                    nc.vector.tensor_scalar_max(relus[j][:, codes, :], by_code[:, codes, :], 0.0)
                else:
                    nc.scalar.activation(relus[j][:, codes, :], by_code[:, codes, :], ACT.Relu)

        def turn_and_square(j):
            e = j * P // C
            if j % 2 == 0:
                h[e] = keep.tile([P, C, PACK], BF16, name="h%d" % e, align_bytes=ALIGN)
            turned = psum.tile([P, PACK, P], F32, name="turned", tag="bank%d" % TURNED_ELSEWHERE.get(j, j))
            for d in range(PACK):
                nc.tensor.transpose(turned[:, d, :], relus[j][:, d, :], ident[:])
            nc.scalar.activation(
                h[e][:, (j % 2) * P : (j % 2 + 1) * P, :], turned[:].rearrange("p d s -> p s d"), ACT.Square
            )

        def quantise(e):
            width = P if e == E - 1 else C
            h_words[e] = keep.tile([P, C], U32, name="h_words", tag=CODES_TAG.get(e, "h_words%d" % e), align_bytes=ALIGN)
            for lo in range(0, C, width):
                slots = slice(e * C + lo, e * C + lo + width)
                nc.vector.quantize_mx(
                    out=h_words[e][:, lo : lo + width].bitcast(FP8X4),
                    scales=h_plane[:, slots],
                    in_=h[e][:, lo : lo + width, :].rearrange("p s d -> p (s d)"),
                )

        def second_layer(e):
            slots = slice(e * C, (e + 1) * C)
            y = psum.tile([P, C], F32, name="y", tag="bank%d" % (TILES - 1 if e == E - 2 else 2 * e))
            nc.tensor.matmul_mx(
                out=y[:],
                lhsT=w2w[e].bitcast(FP4X4),
                lhsT_scale=w2_planes[:, e, :],
                rhs=h_words[e][:].bitcast(FP8X4),
                rhs_scale=h_plane[:, slots],
                start=True,
                stop=True,
            )
            y_sb[e] = keep.tile([P, C], F32, name="y_sb", tag="relu%d" % ((2 * e + 3) % TILES), align_bytes=ALIGN)
            nc.scalar.copy(y_sb[e][:], y[:])

        def scatter(e):
            window = placed[:].indirect(dst_t[:, entries(e * C, (e + 1) * C)])
            nc.vector.tensor_tensor(window, y_sb[e][:], gate_t[:, e * C : (e + 1) * C], MULT)

        for o in range(LAST):
            for g in range(2):
                gather_words(o, g, HALF, "slot_words%d%d" % (o, g))
            for j in range(TILES // 2):
                first_layer(j, o)

        for j in range(TILES // 2):
            gather_last(range(j, j + 1), "last_words%d" % j)
        for j in range(TILES // 2):
            finish_sums(j)

        first_layer(4, 0)

        def hidden(e):
            turn_and_square(2 * e)
            turn_and_square(2 * e + 1)
            quantise(e)

        def results(e):
            second_layer(e)
            scatter(e)

        turn_and_square(0)
        gather_last(range(4, 5), "relu0")
        turn_and_square(1)
        gather_last(range(5, 6), "relu1")
        quantise(0)
        turn_and_square(2)
        gather_last(range(6, 8), "relu2")
        turn_and_square(3)
        first_layer(5, 0)
        first_layer(4, 1)
        finish_sums(4)
        quantise(1)
        first_layer(5, 1)
        finish_sums(5)
        results(0)
        early_passes((6,))
        finish_sums(6)
        hidden(2)
        results(1)
        early_passes((7,))
        finish_sums(7)
        hidden(3)
        results(2)
        results(3)

        nc.sync.dma_start(out[:, 0 : T // 2], placed[:, 0 : T // 2])
        nc.scalar.dma_start(out[:, T // 2 : T], placed[:, T // 2 : T])
